import numpy as np, ml_dtypes
CORES = [10,34,74,98]
N = 4
BF = ml_dtypes.bfloat16
def gentries(a):
    return np.ascontiguousarray(a.reshape(8, 16, -1).transpose(0, 2, 1)).reshape(8, -1)
def gtable(e):
    e = np.asarray(e); return np.ascontiguousarray(e.reshape(8, -1, 16).transpose(0, 2, 1)).reshape(128, -1).astype(np.int32)
P, A, M, Q = 16384, 16, 8, 512
S = N * P
def letters(rng, w, n):
    a = np.add.accumulate(w); return np.searchsorted(a[:-1], rng.random(n) * a[-1], side="right")
def places(rng):
    p = rng.integers(0, S + 1, (N, 8, 2, Q)); u = P // 8
    v = rng.integers(0, 8 * N + 1, p.shape) * u + rng.integers(-1, 2, p.shape)
    p = np.sort(np.where(rng.random(p.shape) < 0.25, np.minimum(np.maximum(v, 0), S), p), axis=2)
    k = (8 * np.arange(N)[:, None] + np.arange(8)) * u
    p[:, :, 0, Q - 5] = k; p[:, :, 1, Q - 5] = k + u; p[:, :, :, Q - 4] = S; p[:, :, :, Q - 3] = 0
    p[:, :, 1, Q - 2] = p[:, :, 0, Q - 2]; p[:, :, 0, Q - 1] = 0; p[:, :, 1, Q - 1] = S
    return p
def pack(s, e, p):
    return {"bwt": np.ascontiguousarray(np.asarray(s).reshape(8, N, P).transpose(1, 0, 2)).astype(np.int32), "pats": np.stack([gtable(e[r].reshape(8, M * Q)) for r in range(N)]), "starts": np.stack([gtable(p[r].reshape(8, 2 * Q)) for r in range(N)])}
def bw(t):
    n = len(t); key = np.zeros(n, np.int64); k = 62 // (A - 1).bit_length()
    for i in range(k): key = key * A + np.roll(t, -i)
    while True:
        o = np.argsort(key); ks = key[o]
        v = np.zeros(n, np.int64); v[o[1:]] = np.add.accumulate((ks[1:] != ks[:-1]).astype(np.int64))
        if v.max() == n - 1 or k >= n: break
        key = (v * n + np.roll(v, -k)) * n + np.roll(v, -2 * k); k *= 3
    return t[o - 1]
def setup_inputs(rng):
    s = []; e = rng.integers(0, A, (N, 8, M, Q)); h = Q // 2
    for g in range(8):
        w = np.exp2(rng.integers(0, 4, A)); c = rng.integers(0, A); w[c] += 4 * A
        s.append(np.concatenate([letters(rng, w * np.exp2(rng.integers(0, 3, A)), P) for r in range(N)]))
        e[:, g, :, :h] = np.where(rng.random((N, M, h)) < 0.875, c, e[:, g, :, :h])
    return pack(np.stack(s), e, places(rng))
def setup_inputs_ends(rng):
    i = np.arange(S); s = np.zeros((8, S), np.int64)
    s[0] = i * A // S; s[1] = A - 1 - s[0]; s[2] = i % A; s[3] = rng.integers(0, A - 1, S); s[4] = rng.integers(1, A, S); s[5] = i // P % A
    s[6] = np.where((i % P == 0) | (i % P == P - 1), A - 1, rng.integers(0, A - 1, S)); s[7] = np.where(i == S - 1, A - 1, rng.integers(0, A - 1, S))
    e = rng.integers(0, A, (N, 8, M, Q)); e[..., 0] = 0; e[..., 1] = A - 1; e[..., 2] = 0; e[:, :, 0, 2] = A - 1; e[..., 3] = 0; e[:, :, M - 1, 3] = A - 1
    q = rng.integers(0, N); e[q] = rng.integers(0, A, (8, M, 1)); e[q, 0] = e[q, 0, 0, 0]
    p = places(rng); p[:, :, 0, :4] = 0; p[:, :, 1, :4] = S; p[q, :, 0] = 0; p[q, :, 1] = S
    return pack(s, e, p)
def setup_inputs_one(rng):
    k = (np.arange(8) + rng.integers(0, A)) % A; c = k[None, :, None, None]
    e = np.where(rng.random((N, 8, 1, Q)) < 0.5, c, rng.integers(0, A, (N, 8, M, Q))); e[..., 0] = k[None, :, None]
    return pack(np.repeat(k[:, None], S, axis=1), e, places(rng))
def setup_inputs_text(rng):
    s = []; e = np.zeros((N, 8, M, Q), np.int64); h = Q // 2
    for g in range(8):
        t = np.tile(letters(rng, np.exp2(rng.integers(0, 3, A)), S // 8), 8); t = np.where(rng.random(S) < 0.03125, rng.integers(0, A, S), t); s.append(bw(t))
        e[:, g] = t[(rng.integers(0, S, (N, 1, Q)) + (M - 1 - np.arange(M))[None, :, None]) % S]
    e[..., h:] = np.where(rng.random((N, 8, M, Q - h)) < 0.0625, rng.integers(0, A, (N, 8, M, Q - h)), e[..., h:])
    p = places(rng); p[:, :, 0, :h] = 0; p[:, :, 1, :h] = S
    return pack(np.stack(s), e, p)
def setup_inputs_spread(rng):
    s = np.stack([np.concatenate([letters(rng, np.exp2(-2.0 * rng.permutation(A)), P) for r in range(N)]) for g in range(8)])
    e = np.stack([s[g][rng.integers(0, S, (N, M, Q))] for g in range(8)], axis=1)
    p = places(rng); p[:, :, 1] = np.minimum(p[:, :, 0] + (rng.integers(0, S + 1, (N, 8, Q)) >> rng.integers(0, 20, (N, 8, Q))), S)
    return pack(s, np.where(rng.random((N, 8, 1, Q)) < 0.5, e, rng.integers(0, A, (N, 8, M, Q))), p)
def check_inputs(d):
    bad = [k + " out of range" for k in ("bwt", "pats") if not ((d[k] >= 0) & (d[k] < A)).all()]
    if not ((d["starts"] >= 0) & (d["starts"] <= S)).all(): bad.append("starts out of range")
    p = np.stack([gentries(a) for a in d["starts"]]).reshape(N, 8, 2, Q)
    if (p[:, :, 0] > p[:, :, 1]).any(): bad.append("lo over hi in starts")
    return bad
def reference(bwt, pats, starts):
    s = bwt.transpose(1, 0, 2).reshape(8, S)
    e = np.stack([gentries(pats[r]) for r in range(N)]).reshape(N, 8, M, Q)
    b = np.stack([gentries(starts[r]) for r in range(N)]).reshape(N, 8, 2, Q).astype(np.int64)
    ends = np.zeros((N, 8, 2, Q), np.int64)
    for g in range(8):
        C = np.array([np.count_nonzero(s[g] < c) for c in range(A)]); occ = np.zeros((A, S + 1), np.int64)
        for c in range(A): occ[c, 1:] = np.add.accumulate((s[g] == c).astype(np.int64))
        p = b[:, g]
        for t in range(M):
            c = e[:, g, t][:, None]; p = C[c] + occ[c, p]
        ends[:, g] = p
    return {"y": np.asarray(np.stack([gtable(ends[r].reshape(8, 2 * Q)) for r in range(N)]), np.float32)}

@@ -1,0 +1,342 @@
+from concourse.bass import DstId, RemoteDMATransfer
+from concourse.mybir import AluOpType as Op, ActivationFunctionType as Fn, AxisListType
+
+R, B = 4, 1024
+NB = R * B
+STR = 4224
+W = 2 * STR
+ASW = 1032
+HC = 384
+
+SCRATCH = {
+    "raw": ("sbuf", [128, 64, 16], "int32"),
+    "half": ("sbuf", [128, 8, 128], "bfloat16"),
+    "let": ("sbuf", [128, B], "bfloat16"),
+    "keyw": ("sbuf", [128, W], "bfloat16"),
+    "base": ("sbuf", [128, W], "bfloat16"),
+    "feat": ("sbuf", [128, 16 * B], "bfloat16"),
+    "sums": ("sbuf", [128, 2 * ASW], "bfloat16"),
+    "hd": ("sbuf", [128, 2 * B], "bfloat16"),
+    "tot": ("sbuf", [128, 2 * 4 * R], "float32"),
+    "rr": ("sbuf", [128, 8], "float32"),
+    "init": ("sbuf", [128, 8], "float32"),
+    "wv": ("sbuf", [128, 2], "float32"),
+    "wd": ("sbuf", [128, 2], "bfloat16"),
+    "gi": ("sbuf", [128, 128], "bfloat16"),
+    "j8": ("sbuf", [128, 128], "bfloat16"),
+    "lp": ("sbuf", [128, 1], "int32"),
+    "li": ("sbuf", [128, 4], "int32"),
+    "lf": ("sbuf", [128, 4], "float32"),
+    "ma": ("sbuf", [128, 128], "bfloat16"),
+    "mb": ("sbuf", [128, 128], "bfloat16"),
+    "bm": ("sbuf", [128, 128], "bfloat16"),
+    "f8": ("sbuf", [128, 128], "bfloat16"),
+    "lfm": ("sbuf", [128, 8 * 128], "bfloat16"),
+    "xq": ("sbuf", [128, 16 * 128], "bfloat16"),
+    "eq": ("sbuf", [128, 16 * 128], "bfloat16"),
+    "idm": ("sbuf", [128, 128], "bfloat16"),
+    "neg": ("sbuf", [128, 128], "bfloat16"),
+    "s2": ("sbuf", [128, 128], "float32"),
+    "s4": ("sbuf", [128, 128], "float32"),
+    "smf": ("sbuf", [128, 128], "float32"),
+    "swf": ("sbuf", [128, 128], "float32"),
+    "smb": ("sbuf", [128, 128], "bfloat16"),
+    "swb": ("sbuf", [128, 128], "bfloat16"),
+    "c8": ("sbuf", [128, 64], "bfloat16"),
+    "pat": ("sbuf", [128, 8, 32], "int32"),
+    "pi": ("sbuf", [128, 8, 32], "int32"),
+    "chi": ("sbuf", [128, 8, 32], "int32"),
+    "cl": ("sbuf", [128, 8, 32], "bfloat16"),
+    "ch2": ("sbuf", [128, 8, 64], "bfloat16"),
+    "clx": ("sbuf", [128, 8 * 512], "bfloat16"),
+    "msk": ("sbuf", [128, 8 * 512], "bfloat16"),
+    "sti": ("sbuf", [128, 64], "int32"),
+    "sf": ("sbuf", [128, 2, 64], "float32"),
+    "oi": ("sbuf", [128, 64], "int32"),
+    "kl": ("sbuf", [128, 2, 64], "bfloat16"),
+    "of0": ("sbuf", [128, 64], "uint16"),
+    "of1": ("sbuf", [128, 64], "uint16"),
+    "kg": ("sbuf", [128, 1024], "bfloat16"),
+    "ym": ("sbuf", [128, 1024], "bfloat16"),
+    "xs": ("sbuf", [128, 1024], "bfloat16"),
+    "yo": ("sbuf", [128, 64], "float32"),
+    "pa": ("psum", [128, 2048], "float32"),
+    "pb": ("psum", [128, 2048], "float32"),
+}
+SEMAPHORES = ["cV", "cS", "cP", "cG", "lpat", "lst", "out", "hk", "hb0", "hb1", "kin", "tin0", "tin1",
+              "bin0", "bin1", "snt"] + ["ld%d" % k for k in range(8)]
+
+
+def helper(rank_core, T, topo):
+    for c in topo.cores_of(rank_core):
+        if topo.die(c) != topo.die(rank_core) and all(topo.may_write(c, d) for d in T.cores if d != rank_core):
+            return c
+
+
+def route(core, to, topo):
+    ids, mask = [], None
+    for c in to:
+        rid, pid = topo.addr(c)[:2]
+        ids.append(DstId(rid=rid, pnc=pid))
+        mask = topo.mask(core, c) if mask is None else mask & topo.mask(core, c)
+    return ids, mask, bin(mask).count("1")
+
+
+def hand_on(g, core, rank, T, topo):
+    ids, mask, width = route(core, [c for c in T.cores if c != T.cores[rank]], topo)
+    came = route(T.cores[rank], [core], topo)[2]
+    sent = 0
+    for buf, at, n, here, there in [(T.keyw, 0, B, "hk", "kin"), (T.base, STR, HC, "hb1", "bin1"), (T.base, 0, HC, "hb0", "bin0")]:
+        piece = buf[:, at + B * rank:at + B * rank + n]
+        g.wait_ge(T.sem[here], came)
+        g.remote_dma_fused([RemoteDMATransfer(dst_ids=ids, dma_engine_mask=mask, remote_sem=T.sem[there],
+                                              srcs=[piece], dsts=[piece for _ in ids], alu_op=0)],
+                           local_sem=T.sem.snt)
+        sent += width
+    g.wait_ge(T.sem.snt, sent)
+
+
+def rank_program(g, core, T, topo):
+    rank = T.rank_of(core)
+    if rank is None:
+        for r, c in enumerate(T.cores):
+            if helper(c, T, topo) == core:
+                hand_on(g, core, r, T, topo)
+        return
+    queues = {"V": g.vector, "S": g.scalar, "P": g.tensor, "G": g, "Y": g.sync}
+    total, seen = {}, {}
+
+    def need(q, deps):
+        for sem, val in deps:
+            if seen.get((q, sem), 0) < val:
+                queues[q].wait_ge(T.sem[sem], val)
+                seen[(q, sem)] = val
+
+    def run(q, deps, f, *a, **kw):
+        need(q, deps)
+        sem = "c" + q
+        f(*a, **kw).then_inc(T.sem[sem], 1)
+        total[sem] = total.get(sem, 0) + 1
+        return (sem, total[sem])
+
+    def dma(q, deps, sem, out, in_):
+        need(q, deps)
+        queues[q].dma_start(out, in_).then_inc(T.sem[sem], 16)
+        total[sem] = total.get(sem, 0) + 16
+        return (sem, total[sem])
+
+    v, s, pe = g.vector, g.scalar, g.tensor
+    others = [c for c in T.cores if c != core]
+    hand = helper(core, T, topo)
+    ids, mask, width = route(core, others, topo)
+    hid, hmask, hwidth = route(core, [hand], topo)
+    hw = route(hand, others, topo)[2]
+    k_in, t_in, b_in = hw * (R - 1), width * (R - 1), (hw + width) * (R - 1)
+
+    def send(deps, piece, sem, to=ids, eng=mask, n=width):
+        need("G", deps)
+        g.remote_dma_fused([RemoteDMATransfer(dst_ids=to, dma_engine_mask=eng, remote_sem=T.sem[sem],
+                                              srcs=[piece], dsts=[piece for _ in to], alu_op=0)],
+                           local_sem=T.sem.snt)
+        total["snt"] = total.get("snt", 0) + n
+
+    ld = []
+    for k in range(8):
+        j, y = k // 2, k % 2
+        ld.append(dma("Y" if k % 2 == 0 else "S", [], "ld%d" % k, T.raw[:, 8 * k:8 * k + 8, :],
+                      T.bwt[y::2, 4096 * j:4096 * j + 4096]))
+    lpat = dma("Y", [], "lpat", T.pat[:, :, :], T.pats[:, :])
+    lst = dma("Y", [], "lst", T.sti[:, :], T.starts[:, :])
+
+    fl = dict(allow_small_or_imprecise_dtypes=True)
+    g_lp = run("G", [], g.iota, T.lp[:, :], [[0, 1]], 0, 1)
+    g_gi = run("G", [], g.iota, T.gi[:, :], [[-16, 8], [0, 16]], 0, 1, **fl)
+    g_j8 = run("G", [], g.iota, T.j8[:, :], [[0, 16], [1, 8]], 1, 0, **fl)
+
+    t_ones = run("V", [], v.memset, T.feat[:, 0:B], 1.0)
+    run("V", [], v.memset, T.sums[:, 0:1], 0.0)
+    run("V", [], v.memset, T.sums[:, ASW:ASW + 1], 0.0)
+    run("V", [], v.memset, T.tot[:, 4 * rank:4 * rank + 4], 0.0)
+    run("V", [], v.memset, T.tot[:, 4 * (R + rank):4 * (R + rank) + 4], 0.0)
+    t_rr = run("V", [], v.memset, T.rr[:, :], 0.0)
+    run("V", [g_lp], v.tensor_scalar, T.li[:, 0:1], T.lp[:, :], 15, None, Op.bitwise_and)
+    run("V", [], v.tensor_scalar, T.li[:, 1:2], T.lp[:, :], 7, None, Op.bitwise_and)
+    t = run("V", [], v.tensor_scalar, T.li[:, 2:3], T.lp[:, :], 3, 1, Op.arith_shift_right, Op.bitwise_and)
+    run("V", [g_gi], v.tensor_scalar, T.ma[:, :], T.gi[:, :], 0.0, None, Op.is_ge)
+    t2 = run("V", [], v.tensor_scalar, T.mb[:, :], T.gi[:, :], 15.0, None, Op.is_le)
+    run("V", [t], v.tensor_scalar, T.lf[:, 0:1], T.li[:, 0:1], 0.0625, None, Op.mult)
+    t_lane = run("V", [], v.tensor_copy, T.lf[:, 1:3], T.li[:, 1:3])
+    t3 = run("V", [t2], v.tensor_tensor, T.bm[:, :], T.ma[:, :], T.mb[:, :], Op.mult)
+    run("V", [g_j8], v.tensor_scalar, T.s2[:, :], T.j8[:, :], 8.0, None, Op.is_lt)
+    t_s24 = run("V", [], v.tensor_scalar, T.s4[:, :], T.j8[:, :], 8.0, None, Op.is_ge)
+    t4 = run("V", [t3], v.tensor_tensor, T.f8[:, :], T.bm[:, :], T.j8[:, :], Op.mult)
+    for y in range(8):
+        t_lfm = run("V", [t4], v.tensor_scalar, T.lfm[:, 128 * y:128 * y + 128], T.f8[:, :], float(y + 1), 2.0, Op.is_equal, Op.mult)
+    run("G", [t_s24], g.affine_select, T.smf[:, :], T.s2[:, :], [[-1, 128]], Op.is_equal, 0.0, -1, 1)
+    g_sh = run("G", [], g.affine_select, T.swf[:, :], T.s4[:, :], [[-1, 128]], Op.is_equal, 0.0, 7, 1)
+    g_id = run("G", [t_ones], g.affine_select, T.idm[:, :], T.feat[:, 0:128], [[-1, 128]], Op.is_equal, 0.0, 0, 1)
+    run("S", [t_ones], s.activation, T.c8[:, 0:32], T.feat[:, 0:32], Fn.Copy, scale=0.46875)
+    run("S", [], s.activation, T.c8[:, 32:64], T.feat[:, 0:32], Fn.Copy, scale=-0.03125)
+    run("S", [g_sh], s.activation, T.smb[:, :], T.smf[:, :], Fn.Copy)
+    t_sh = run("S", [], s.activation, T.swb[:, :], T.swf[:, :], Fn.Copy)
+    t_neg = run("S", [g_id], s.activation, T.neg[:, :], T.idm[:, :], Fn.Copy, scale=-1.0)
+
+    for k in range(8):
+        j, y = k // 2, k % 2
+        t = run("V", [ld[k]], v.tensor_copy, T.half[:, :, 32 * j + 16 * y:32 * j + 16 * y + 16], T.raw[:, 8 * k:8 * k + 8, :])
+    for i in range(8):
+        t_let = run("V", [t], v.transpose, T.let[:, i::8], T.half[:, i, :])
+    t_key = run("V", [t_let, t_lane], v.tensor_scalar, T.keyw[:, B * rank:B * rank + B], T.let[:, :], T.lf[:, 0:1], None, Op.add)
+    send([t_key], T.keyw[:, B * rank:B * rank + B], "hk", hid, hmask, hwidth)
+    run("G", [], g.affine_select, T.xq[:, 0:1024], T.feat[:, 0:1024], [[-1, 8], [-16, 8], [0, 16]], Op.is_equal, 0.0, 0, 1)
+    g_xq = run("G", [], g.affine_select, T.xq[:, 1024:2048], T.feat[:, 0:1024], [[-1, 8], [-16, 8], [0, 16]], Op.is_equal, 0.0, -8, 1)
+
+    t_f = {0: t_ones}
+    for c in list(range(8, 16)) + list(range(1, 8)):
+        t_f[c] = run("V", [], v.tensor_scalar, T.feat[:, B * c:B * c + B], T.let[:, :], float(c), None, Op.is_ge)
+    t_b, t_s, t_ini, t_v = {}, {}, {}, {}
+
+    def count(chi):
+        for c in range(8 * chi, 8 * chi + 8):
+            for h in range(2):
+                at = B * chi + 512 * h
+                t = run("P", [t_f[c], t_lfm], pe.matmul, T.pa[:, at:at + 512], T.lfm[:, 128 * (c % 8):128 * (c % 8) + 128],
+                        T.feat[:, B * c + 512 * h:B * c + 512 * h + 512], c % 8 == 0, c % 8 == 7)
+        return t
+
+    def own(chi):
+        return 4 * (R * chi + rank)
+
+    def shifted(chi, deps):
+        for h in range(2):
+            out = T.pb[:, B * chi + 512 * h:B * chi + 512 * h + 512]
+            t_b[chi] = run("P", t_s[chi] + [t_sh] + deps, pe.matmul, out, T.smb[:, :],
+                           T.sums[:, ASW * chi + 512 * h:ASW * chi + 512 * h + 512], True, chi == 1)
+            if chi == 0:
+                t_b[chi] = run("P", [], pe.matmul, out, T.swb[:, :], T.sums[:, ASW + 512 * h:ASW + 512 * h + 512], False, True)
+
+    def begin(chi, bank, deps):
+        col, lo, mid, hi = 4 * chi, 4 * R * chi, own(chi), 4 * R * (chi + 1)
+        need("V", [("tin%d" % chi, t_in), t_rr] + t_s[chi])
+        if rank:
+            run("V", [], v.tensor_reduce, T.rr[:, col:col + 1], T.tot[:, lo:mid], AxisListType.X, Op.add)
+        t_t = run("V", [], v.tensor_reduce, T.rr[:, col + 1:col + 2], T.tot[:, lo:hi], AxisListType.X, Op.add)
+        t = run("V", [], v.tensor_reduce, T.init[:, col:col + 1], T.tot[:, mid:hi], AxisListType.X, Op.add, negate=True)
+        pt = T.pb[:, 512 * bank:512 * bank + 2]
+        t_pt = run("P", [t_t, t_sh, g_sh] + deps, pe.matmul, pt, T.smf[:, :], T.rr[:, col:col + 2], True, chi == 1)
+        if chi == 0:
+            t_pt = run("P", [], pe.matmul, pt, T.swf[:, :], T.rr[:, 4:6], False, True)
+        t = run("V", [t], v.tensor_scalar, T.init[:, col + 1:col + 2], T.init[:, col:col + 1], float(2 * (16 * NB - 16)), None, Op.add)
+        t_ini[chi] = run("V", [t, t_pt], v.tensor_tensor, T.init[:, col + 2:col + 3], T.init[:, col + 1:col + 2], pt[:, 0:1], Op.subtract)
+        t_v[chi] = run("V", [], v.tensor_scalar, T.wv[:, chi:chi + 1], pt[:, 1:2], -1.0, float(2 * 16 * NB), Op.mult, Op.add)
+
+    def table(chi):
+        t_sc, start, t_hd = t_ini[chi], T.init[:, 4 * chi + 2:4 * chi + 3], []
+        for h in range(2):
+            at, sc = B * chi + 512 * h, ASW * chi + 1 + 512 * h
+            t_sc = run("V", [t_sc, t_b[chi]] + t_s[chi], v.tensor_tensor_scan, T.pa[:, at:at + 512], T.sums[:, sc:sc + 512],
+                       T.pb[:, at:at + 512], start, Op.add, Op.subtract)
+            if h == 0:
+                start = T.init[:, 4 * chi + 3:4 * chi + 4]
+                t_sc = run("V", [t_sc], v.tensor_copy, start, T.pa[:, at + 511:at + 512])
+            t_hd.append(run("S", [t_sc, t_lane], s.activation, T.hd[:, at:at + 512], T.pa[:, at:at + 512], Fn.Copy, scale=T.lf[:, 2:3]))
+        for h, (a, e) in enumerate([(0, HC), (HC, B)]):
+            at, to = B * chi, STR * chi + B * rank
+            t = run("V", [t_hd[h]], v.tensor_tensor, T.base[:, to + a:to + e], T.pa[:, at + a:at + e], T.hd[:, at + a:at + e], Op.subtract)
+            if h == 0:
+                send([t], T.base[:, to + a:to + e], "hb%d" % chi, hid, hmask, hwidth)
+            else:
+                send([t], T.base[:, to + a:to + e], "bin%d" % chi)
+        return t
+
+    def total_of(chi):
+        return T.tot[:, own(chi):own(chi) + 1]
+
+    t = count(1)
+    t_s[1] = [run("S", [t, t_ones, t_rr], s.activation, T.sums[:, ASW + 1:ASW + 1 + B], T.pa[:, B:2 * B], Fn.Copy, accum_out=total_of(1))]
+    send(t_s[1], T.tot[:, own(1):own(1) + 4], "tin1")
+    t = count(0)
+    t_s0 = run("S", [t], s.activation, T.sums[:, 1:513], T.pa[:, 0:512], Fn.Copy, accum_out=total_of(0))
+    t_s1 = run("V", [t], v.tensor_reduce, T.tot[:, own(0) + 1:own(0) + 2], T.pa[:, 512:1024], AxisListType.X, Op.add)
+    send([t_s0, t_s1], T.tot[:, own(0):own(0) + 4], "tin0")
+    t_s[0] = [t_s0, run("V", [], v.tensor_copy, T.sums[:, 513:1025], T.pa[:, 512:1024])]
+    shifted(1, [])
+    begin(1, 0, [])
+    table(1)
+    shifted(0, [t_v[1]])
+    begin(0, 2, [t_v[1], t_b[1]])
+    t_tab = table(0)
+
+    run("V", [], v.memset, T.keyw[:, NB:STR], 1024.0)
+    run("V", [], v.memset, T.base[:, NB:STR], 0.0)
+    t_pad = run("V", [], v.memset, T.base[:, STR + NB:W], 0.0)
+    t = run("V", [t_v[0]], v.tensor_scalar, T.wd[:, :], T.wv[:, :], T.lf[:, 2:3], None, Op.mult)
+    run("V", [lpat], v.tensor_scalar, T.pi[:, :, :], T.pat[:, :, :], 7, None, Op.bitwise_and)
+    t_ci = run("V", [], v.tensor_scalar, T.chi[:, :, :], T.pat[:, :, :], 3, None, Op.arith_shift_right)
+    t_end = run("V", [t, t_pad], v.tensor_tensor, T.base[:, NB:W:STR], T.wv[:, :], T.wd[:, :], Op.subtract)
+    t_cl = run("V", [t_ci], v.tensor_copy, T.cl[:, :, :], T.pi[:, :, :])
+    for h in range(2):
+        t_ch = run("V", [], v.tensor_scalar, T.ch2[:, :, 32 * h:32 * h + 32], T.chi[:, :, :], float(STR), None, Op.mult)
+    t_c, t_m = {}, {}
+    for st in range(8):
+        bank = st % 4
+        deps = [t_cl, g_xq, t_tab] + ([t_c[st - 4]] if st >= 4 else [])
+        for q in range(16):
+            lo = 512 * bank + q
+            t = run("P", deps, pe.matmul, T.pa[:, lo:512 * bank + 512:16], T.xq[:, 128 * q:128 * q + 128], T.cl[:, st, :], True, True)
+        t_c[st] = run("S", [t], s.activation, T.clx[:, 512 * st:512 * st + 512], T.pa[:, 512 * bank:512 * bank + 512], Fn.Copy)
+        if st == 3:
+            for q in range(16):
+                t = run("P", [g_id], pe.matmul, T.pb[:, 128 * q:128 * q + 128], T.xq[:, 128 * q:128 * q + 128], T.idm[:, :], True, True)
+            for i in range(4):
+                t_eq = run("S", [t], s.activation, T.eq[:, 512 * i:512 * i + 512], T.pb[:, 512 * i:512 * i + 512], Fn.Copy, scale=0.03125)
+    t = run("V", [lst], v.tensor_scalar, T.sf[:, 0, :], T.sti[:, :], 0.0625, -0.03125, Op.mult, Op.add)
+    t = run("V", [t, t_ch], v.tensor_tensor, T.sf[:, 1, :], T.sf[:, 0, :], T.ch2[:, 0, :], Op.add)
+    t_of = run("V", [t], v.tensor_scalar, T.of0[:, :], T.sf[:, 1, :], -0.4375, None, Op.add)
+    t = run("V", [], v.tensor_scalar, T.oi[:, :], T.sf[:, 1, :], -0.4375, None, Op.add)
+    t_kl = run("V", [t], v.tensor_tensor, T.kl[:, 0, :], T.sf[:, 1, :], T.oi[:, :], Op.subtract)
+    for st in range(8):
+        t_m[st] = run("V", [t_c[st], t_lane], v.tensor_scalar, T.msk[:, 512 * st:512 * st + 512], T.clx[:, 512 * st:512 * st + 512],
+                      T.lf[:, 1:2], None, Op.is_equal)
+        if st == 3:
+            t_dup = run("V", [("kin", k_in), t_pad], v.tensor_scalar, T.keyw[:, STR:W], T.keyw[:, 0:STR], -8.0, None, Op.add)
+
+    of = [T.of0, T.of1]
+    pend = [("bin1", b_in), ("bin0", b_in), t_end]
+    ps = [T.pa[:, 1024:1088], T.pa[:, 1536:1600]]
+    free = [t_c[7], t_eq, t_ch, t_neg]
+    for st in range(8):
+        o, P = of[st % 2], ps[st % 2]
+        for h in range(2):
+            run("P", free, pe.matmul, T.pa[:, 512 * h:512 * h + 512], T.idm[:, :], T.clx[:, 512 * st:512 * st + 512], True, False)
+        run("P", [], pe.matmul, P, T.idm[:, :], T.c8[:, :], True, False)
+        if st < 7:
+            run("P", [], pe.matmul, P, T.idm[:, :], T.ch2[:, st + 1, :], False, False)
+        t_kg, t_y, t_ym = [], [], []
+        for h in range(2):
+            t_kg.append(run("S", [t_of, t_dup], s.activation, T.kg[:, 512 * h:512 * h + 512],
+                            T.keyw[:, 0:W].indirect(o[:, 32 * h:32 * h + 32]), Fn.Copy))
+            t_ym.append(run("V", [t_of, t_m[st]] + pend, v.tensor_tensor, T.ym[:, 512 * h:512 * h + 512],
+                            T.base[:, 0:W].indirect(o[:, 32 * h:32 * h + 32]), T.msk[:, 512 * st:512 * st + 512], Op.mult))
+        for h in range(2):
+            for q in range(16):
+                run("P", [t_kl], pe.matmul, T.pa[:, 512 * h + q:512 * h + 512:16], T.xq[:, 128 * q:128 * q + 128],
+                    T.kl[:, st % 2, 32 * h:32 * h + 32], False, False)
+            t_y.append(run("P", [t_kg[h]], pe.matmul, T.pa[:, 512 * h:512 * h + 512], T.neg[:, :], T.kg[:, 512 * h:512 * h + 512], False, True))
+        t_xa = run("S", [t_y[0]], s.activation, T.xs[:, 0:512], T.pa[:, 0:512], Fn.Sign)
+        t_xb = run("V", [t_y[1]], v.tensor_scalar, T.xs[:, 512:1024], T.pa[:, 512:1024], 0.0, 2.0, Op.is_gt, Op.mult)
+        for q in range(16):
+            run("P", [t_ym[1]], pe.matmul, P, T.eq[:, 128 * q:128 * q + 128], T.ym[:, q::16], False, False)
+        for q in range(16):
+            t_p = run("P", [t_xa, t_xb], pe.matmul, P, T.eq[:, 128 * q:128 * q + 128], T.xs[:, q::16], False, q == 15)
+        free = []
+        if st < 7:
+            t_of = run("V", [t_p], v.tensor_scalar, of[1 - st % 2][:, :], P, -0.4375, None, Op.add)
+            t = run("V", [], v.tensor_scalar, T.oi[:, :], P, -0.4375, None, Op.add)
+            t_kl = run("V", [t], v.tensor_tensor, T.kl[:, 1 - st % 2, :], P, T.oi[:, :], Op.subtract)
+        else:
+            t = run("V", [t_p], v.tensor_scalar, T.yo[:, :], P, 16.0, 0.5, Op.mult, Op.add)
+            dma("Y", [t], "out", T.y[:, :], T.yo[:, :])
+
+    for sem in ["cV", "cS", "cP", "cG", "out", "snt"]:
+        need("G", [(sem, total[sem])])

@@ -1,3 +1,4 @@
+import math
 from concourse.bass import DstId, RemoteDMATransfer
 from concourse.mybir import AluOpType as Op, ActivationFunctionType as Fn, AxisListType
 
@@ -5,72 +6,102 @@ R, B = 4, 1024
 NB = R * B
 STR = 4224
 W = 2 * STR
-ASW = 1032
-HC = 384
+KD = 256
+HC = 448
+EARLY, MASKS = 4, 1
+DUP = "YVS"
+BIG = 131072.0
+SEL = 16384.0
+PARTS = [(0, HC, 0, HC // 8, HC // 8 + HC),
+         (HC, B + 1 - HC, HC // 8 + HC, HC // 8 + HC + (B - HC) // 8 + 8, HC // 8 + HC + (B - HC) // 8 + B - HC + 16)]
+SW = PARTS[1][4]
+ZW = max(HC, B - HC) + 8
+SHARE = [[("V", 0, 2), ("S", 1, 2)], [("S", 0, 1)]]
 
+bf, f32, i32 = "bfloat16", "float32", "int32"
 SCRATCH = {
-    "raw": ("sbuf", [128, 64, 16], "int32"),
-    "half": ("sbuf", [128, 8, 128], "bfloat16"),
-    "let": ("sbuf", [128, B], "bfloat16"),
-    "keyw": ("sbuf", [128, W], "bfloat16"),
-    "base": ("sbuf", [128, W], "bfloat16"),
-    "feat": ("sbuf", [128, 16 * B], "bfloat16"),
-    "sums": ("sbuf", [128, 2 * ASW], "bfloat16"),
-    "hd": ("sbuf", [128, 2 * B], "bfloat16"),
-    "tot": ("sbuf", [128, 2 * 4 * R], "float32"),
-    "rr": ("sbuf", [128, 8], "float32"),
-    "init": ("sbuf", [128, 8], "float32"),
-    "wv": ("sbuf", [128, 2], "float32"),
-    "wd": ("sbuf", [128, 2], "bfloat16"),
-    "gi": ("sbuf", [128, 128], "bfloat16"),
-    "j8": ("sbuf", [128, 128], "bfloat16"),
-    "lp": ("sbuf", [128, 1], "int32"),
-    "li": ("sbuf", [128, 4], "int32"),
-    "lf": ("sbuf", [128, 4], "float32"),
-    "ma": ("sbuf", [128, 128], "bfloat16"),
-    "mb": ("sbuf", [128, 128], "bfloat16"),
-    "bm": ("sbuf", [128, 128], "bfloat16"),
-    "f8": ("sbuf", [128, 128], "bfloat16"),
-    "lfm": ("sbuf", [128, 8 * 128], "bfloat16"),
-    "xq": ("sbuf", [128, 16 * 128], "bfloat16"),
-    "eq": ("sbuf", [128, 16 * 128], "bfloat16"),
-    "idm": ("sbuf", [128, 128], "bfloat16"),
-    "neg": ("sbuf", [128, 128], "bfloat16"),
-    "s2": ("sbuf", [128, 128], "float32"),
-    "s4": ("sbuf", [128, 128], "float32"),
-    "smf": ("sbuf", [128, 128], "float32"),
-    "swf": ("sbuf", [128, 128], "float32"),
-    "smb": ("sbuf", [128, 128], "bfloat16"),
-    "swb": ("sbuf", [128, 128], "bfloat16"),
-    "c8": ("sbuf", [128, 64], "bfloat16"),
-    "pat": ("sbuf", [128, 8, 32], "int32"),
-    "pi": ("sbuf", [128, 8, 32], "int32"),
-    "chi": ("sbuf", [128, 8, 32], "int32"),
-    "cl": ("sbuf", [128, 8, 32], "bfloat16"),
-    "ch2": ("sbuf", [128, 8, 64], "bfloat16"),
-    "clx": ("sbuf", [128, 8 * 512], "bfloat16"),
-    "msk": ("sbuf", [128, 8 * 512], "bfloat16"),
-    "sti": ("sbuf", [128, 64], "int32"),
-    "sf": ("sbuf", [128, 2, 64], "float32"),
-    "oi": ("sbuf", [128, 64], "int32"),
-    "kl": ("sbuf", [128, 2, 64], "bfloat16"),
-    "of0": ("sbuf", [128, 64], "uint16"),
-    "of1": ("sbuf", [128, 64], "uint16"),
-    "kg": ("sbuf", [128, 1024], "bfloat16"),
-    "ym": ("sbuf", [128, 1024], "bfloat16"),
-    "xs": ("sbuf", [128, 1024], "bfloat16"),
-    "yo": ("sbuf", [128, 64], "float32"),
-    "pa": ("psum", [128, 2048], "float32"),
-    "pb": ("psum", [128, 2048], "float32"),
+    "raw": ("sbuf", [128, 64, 16], i32),
+    "half": ("sbuf", [128, 8, 128], bf),
+    "let": ("sbuf", [128, B], bf),
+    "pw": ("sbuf", [128, B], bf),
+    "feat": ("sbuf", [128, 4 * B], bf),
+    "hq": ("sbuf", [128, B], i32),
+    "nn": ("sbuf", [128, B], bf),
+    "keyw": ("sbuf", [128, W], bf),
+    "base": ("sbuf", [128, W], bf),
+    "ship": ("sbuf", [128, R * SW], bf),
+    "zt": ("sbuf", [128, 6 * ZW], bf),
+    "vr": ("sbuf", [128, 132], f32),
+    "tot": ("sbuf", [128, 4 * R], f32),
+    "init": ("sbuf", [128, 1], f32),
+    "hb": ("sbuf", [128, 130], bf),
+    "rb": ("sbuf", [128, 130], bf),
+    "ones": ("sbuf", [128, ZW], bf),
+    "onef": ("sbuf", [128, 128], f32),
+    "c32": ("sbuf", [128, 128], bf),
+    "lp": ("sbuf", [128, 1], i32),
+    "li": ("sbuf", [128, 8], i32),
+    "lf": ("sbuf", [128, 24], f32),
+    "m16": ("sbuf", [128, 128], bf),
+    "wx": ("sbuf", [128, 128], bf),
+    "wb": ("sbuf", [128, 128], bf),
+    "wj": ("sbuf", [128, 4 * 128], bf),
+    "t1": ("sbuf", [128, 128], bf),
+    "t2": ("sbuf", [128, 128], bf),
+    "t3": ("sbuf", [128, 128], f32),
+    "bm": ("sbuf", [128, 128], bf),
+    "b32": ("sbuf", [128, 128], bf),
+    "b16": ("sbuf", [128, 128], bf),
+    "kap": ("sbuf", [128, 10], f32),
+    "oh": ("sbuf", [128, 8], f32),
+    "gm": ("sbuf", [128, 128], bf),
+    "g1": ("sbuf", [128, 128], bf),
+    "nm": ("sbuf", [128, 128], bf),
+    "lt": ("sbuf", [128, 128], f32),
+    "le": ("sbuf", [128, 128], f32),
+    "idm": ("sbuf", [128, 128], bf),
+    "neg": ("sbuf", [128, 128], bf),
+    "swp": ("sbuf", [128, 128], bf),
+    "nsw": ("sbuf", [128, 128], bf),
+    "wu": ("sbuf", [128, 2 * 128], bf),
+    "xq": ("sbuf", [128, 8 * 128], bf),
+    "e16": ("sbuf", [128, 8 * 128], bf),
+    "e32": ("sbuf", [128, 8 * 128], bf),
+    "ck": ("sbuf", [128, 512], bf),
+    "zr": ("sbuf", [128, 512], bf),
+    "zs": ("sbuf", [128, 64], f32),
+    "no": ("sbuf", [128, 128], f32),
+    "pat": ("sbuf", [128, 256], i32),
+    "cl": ("sbuf", [128, 256], bf),
+    "cd": ("sbuf", [128, 512], bf),
+    "ch": ("sbuf", [128, 512], bf),
+    "clb": ("sbuf", [128, 2 * 512], f32),
+    "ab": ("sbuf", [128, 8 * 512], bf),
+    "msk": ("sbuf", [128, 8 * 512], bf),
+    "sti": ("sbuf", [128, 64], i32),
+    "s1": ("sbuf", [128, 64], i32),
+    "s2": ("sbuf", [128, 64], i32),
+    "s3": ("sbuf", [128, 32], f32),
+    "s4": ("sbuf", [128, 64], f32),
+    "kc": ("sbuf", [128, 64], bf),
+    "sel": ("sbuf", [128, 128], f32),
+    "oi": ("sbuf", [128, 128], i32),
+    "kl": ("sbuf", [128, 128], bf),
+    "off": ("sbuf", [128, 128], "uint16"),
+    "kg": ("sbuf", [128, 1024], bf),
+    "ym": ("sbuf", [128, 1024], bf),
+    "xs": ("sbuf", [128, 1024], bf),
+    "yo": ("sbuf", [128, 64], f32),
+    "pa": ("psum", [128, 2048], f32),
+    "pb": ("psum", [128, 2048], f32),
 }
-SEMAPHORES = ["cV", "cS", "cP", "cG", "lpat", "lst", "out", "hk", "hb0", "hb1", "kin", "tin0", "tin1",
-              "bin0", "bin1", "snt"] + ["ld%d" % k for k in range(8)]
+SEMAPHORES = (["cV", "cS", "cP", "cG", "lpat", "lst", "out", "hk", "hl", "tin", "snt", "dup"] + ["ld%d" % k for k in range(8)]
+              + ["%s%d" % (n, r) for n in ("kin", "la", "lb") for r in range(R)])
 
 
-def helper(rank_core, T, topo):
-    for c in topo.cores_of(rank_core):
-        if topo.die(c) != topo.die(rank_core) and all(topo.may_write(c, d) for d in T.cores if d != rank_core):
-            return c
+def helpers(rank_core, T, topo):
+    return [c for c in topo.cores_of(rank_core)
+            if topo.die(c) != topo.die(rank_core) and all(topo.may_write(c, d) for d in T.cores if d != rank_core)]
 
 
 def route(core, to, topo):
@@ -82,25 +113,42 @@ def route(core, to, topo):
     return ids, mask, bin(mask).count("1")
 
 
+def halves(mask, n):
+    bits = [e for e in range(mask.bit_length()) if mask >> e & 1]
+    k = len(bits) // n
+    return [sum(1 << e for e in bits[k * i:k * i + k]) for i in range(n)]
+
+
+def inside(home, hands, T, topo):
+    away = route(home, [c for c in T.cores if c != home], topo)[1]
+    return halves(route(home, hands, topo)[1] & ~away, len(hands))
+
+
+def relayed(T, rank, i, n):
+    kw, lw = (B - KD) // n, PARTS[0][4] // n
+    ka, la = B * rank + KD + kw * i, SW * rank + lw * i
+    return T.keyw[:, ka:ka + kw], T.ship[:, la:la + lw]
+
+
 def hand_on(g, core, rank, T, topo):
-    ids, mask, width = route(core, [c for c in T.cores if c != T.cores[rank]], topo)
-    came = route(T.cores[rank], [core], topo)[2]
-    sent = 0
-    for buf, at, n, here, there in [(T.keyw, 0, B, "hk", "kin"), (T.base, STR, HC, "hb1", "bin1"), (T.base, 0, HC, "hb0", "bin0")]:
-        piece = buf[:, at + B * rank:at + B * rank + n]
+    home = T.cores[rank]
+    hands = helpers(home, T, topo)
+    ids, mask, width = route(core, [T.cores[(rank + k) % R] for k in range(1, R)], topo)
+    came = bin(inside(home, hands, T, topo)[0]).count("1")
+    pieces = relayed(T, rank, hands.index(core), len(hands))
+    for piece, here, there in zip(pieces, ["hk", "hl"], ["kin%d" % rank, "la%d" % rank]):
         g.wait_ge(T.sem[here], came)
         g.remote_dma_fused([RemoteDMATransfer(dst_ids=ids, dma_engine_mask=mask, remote_sem=T.sem[there],
                                               srcs=[piece], dsts=[piece for _ in ids], alu_op=0)],
                            local_sem=T.sem.snt)
-        sent += width
-    g.wait_ge(T.sem.snt, sent)
+    g.wait_ge(T.sem.snt, 2 * width)
 
 
 def rank_program(g, core, T, topo):
     rank = T.rank_of(core)
     if rank is None:
         for r, c in enumerate(T.cores):
-            if helper(c, T, topo) == core:
+            if core in helpers(c, T, topo):
                 hand_on(g, core, r, T, topo)
         return
     queues = {"V": g.vector, "S": g.scalar, "P": g.tensor, "G": g, "Y": g.sync}
@@ -126,217 +174,383 @@ def rank_program(g, core, T, topo):
         return (sem, total[sem])
 
     v, s, pe = g.vector, g.scalar, g.tensor
-    others = [c for c in T.cores if c != core]
-    hand = helper(core, T, topo)
-    ids, mask, width = route(core, others, topo)
-    hid, hmask, hwidth = route(core, [hand], topo)
-    hw = route(hand, others, topo)[2]
-    k_in, t_in, b_in = hw * (R - 1), width * (R - 1), (hw + width) * (R - 1)
 
-    def send(deps, piece, sem, to=ids, eng=mask, n=width):
+    def ts(deps, *a):
+        return run("V", deps, v.tensor_scalar, *a)
+
+    def tt(deps, *a):
+        return run("V", deps, v.tensor_tensor, *a)
+
+    def act(deps, *a, **kw):
+        return run("S", deps, s.activation, *a, **kw)
+
+    def mm(deps, *a):
+        return run("P", deps, pe.matmul, *a)
+
+    def pick(deps, *a):
+        return run("G", deps, g.affine_select, *a)
+
+    def mat(buf, k):
+        return buf[:, 128 * k:128 * k + 128]
+
+    def bank(k):
+        return (T.pa if k < 4 else T.pb)[:, 512 * (k % 4):512 * (k % 4) + 512]
+
+    others = [T.cores[(rank + k) % R] for k in range(1, R)]
+    hands = helpers(core, T, topo)
+    ids, mask, width = route(core, others, topo)
+    hids, hmasks = route(core, hands, topo)[0], inside(core, hands, T, topo)
+    hwidth = bin(sum(hmasks)).count("1")
+    hw = len(hands) * route(hands[0], others, topo)[2]
+
+    def send(deps, src, dst, sem):
         need("G", deps)
-        g.remote_dma_fused([RemoteDMATransfer(dst_ids=to, dma_engine_mask=eng, remote_sem=T.sem[sem],
-                                              srcs=[piece], dsts=[piece for _ in to], alu_op=0)],
-                           local_sem=T.sem.snt)
-        total["snt"] = total.get("snt", 0) + n
+        g.remote_dma_fused([RemoteDMATransfer(dst_ids=ids, dma_engine_mask=mask, remote_sem=T.sem[sem],
+                                              srcs=[src], dsts=[dst for _ in ids], alu_op=0)], local_sem=T.sem.snt)
+        total["snt"] = total.get("snt", 0) + width
+
+    def leave(deps, which, sem):
+        need("G", deps)
+        parts = [relayed(T, rank, i, len(hands))[which] for i in range(len(hands))]
+        g.remote_dma_fused([RemoteDMATransfer(dst_ids=[hids[i]], dma_engine_mask=hmasks[i], remote_sem=T.sem[sem],
+                                              srcs=[p], dsts=[p], alu_op=0) for i, p in enumerate(parts)], local_sem=T.sem.snt)
+        total["snt"] = total.get("snt", 0) + hwidth
 
     ld = []
     for k in range(8):
         j, y = k // 2, k % 2
         ld.append(dma("Y" if k % 2 == 0 else "S", [], "ld%d" % k, T.raw[:, 8 * k:8 * k + 8, :],
                       T.bwt[y::2, 4096 * j:4096 * j + 4096]))
-    lpat = dma("Y", [], "lpat", T.pat[:, :, :], T.pats[:, :])
+    lpat = dma("Y", [], "lpat", T.pat[:, :], T.pats[:, :])
     lst = dma("Y", [], "lst", T.sti[:, :], T.starts[:, :])
 
     fl = dict(allow_small_or_imprecise_dtypes=True)
+    one = T.ones[:, 0:128]
     g_lp = run("G", [], g.iota, T.lp[:, :], [[0, 1]], 0, 1)
-    g_gi = run("G", [], g.iota, T.gi[:, :], [[-16, 8], [0, 16]], 0, 1, **fl)
-    g_j8 = run("G", [], g.iota, T.j8[:, :], [[0, 16], [1, 8]], 1, 0, **fl)
+    g_m16 = run("G", [], g.iota, T.m16[:, :], [[0, 8], [1, 16]], 1, 0, **fl)
+    t_one = run("V", [], v.memset, T.ones[:, :], 1.0)
+    run("V", [], v.memset, T.onef[:, :], 1.0)
+    t_c32 = run("V", [], v.memset, T.c32[:, :], 32.0)
+    t = pick([t_one], T.t1[:, :], one, [[-16, 8], [0, 16]], Op.is_ge, 0.0, 0, 1)
+    g_bm = pick([t], T.bm[:, :], T.t1[:, :], [[16, 8], [0, 16]], Op.is_ge, 0.0, 15, -1)
+    g_id = pick([], T.idm[:, :], one, [[-1, 128]], Op.is_equal, 0.0, 0, 1)
+    t = pick([t_c32], T.t2[:, :], T.c32[:, :], [[-1, 128]], Op.is_ge, 0.0, 0, 1)
+    g_gm = pick([t], T.gm[:, :], T.t2[:, :], [[4, 32], [0, 4]], Op.is_ge, 0.0, 3, -1)
+    s_wx = act([g_m16], T.wx[:, :], T.m16[:, :], Fn.Exp, scale=-math.log(32.0))
 
-    t_ones = run("V", [], v.memset, T.feat[:, 0:B], 1.0)
-    run("V", [], v.memset, T.sums[:, 0:1], 0.0)
-    run("V", [], v.memset, T.sums[:, ASW:ASW + 1], 0.0)
-    run("V", [], v.memset, T.tot[:, 4 * rank:4 * rank + 4], 0.0)
-    run("V", [], v.memset, T.tot[:, 4 * (R + rank):4 * (R + rank) + 4], 0.0)
-    t_rr = run("V", [], v.memset, T.rr[:, :], 0.0)
+    lf = {n: T.lf[:, k:k + 1] for k, n in enumerate(
+        ["lane", "y", "u", "i", "x16", "ym4", "u1", "bu", "bu1", "tc", "d0", "top", "d", "d8", "sl", "zs"])}
     run("V", [g_lp], v.tensor_scalar, T.li[:, 0:1], T.lp[:, :], 15, None, Op.bitwise_and)
-    run("V", [], v.tensor_scalar, T.li[:, 1:2], T.lp[:, :], 7, None, Op.bitwise_and)
-    t = run("V", [], v.tensor_scalar, T.li[:, 2:3], T.lp[:, :], 3, 1, Op.arith_shift_right, Op.bitwise_and)
-    run("V", [g_gi], v.tensor_scalar, T.ma[:, :], T.gi[:, :], 0.0, None, Op.is_ge)
-    t2 = run("V", [], v.tensor_scalar, T.mb[:, :], T.gi[:, :], 15.0, None, Op.is_le)
-    run("V", [t], v.tensor_scalar, T.lf[:, 0:1], T.li[:, 0:1], 0.0625, None, Op.mult)
-    t_lane = run("V", [], v.tensor_copy, T.lf[:, 1:3], T.li[:, 1:3])
-    t3 = run("V", [t2], v.tensor_tensor, T.bm[:, :], T.ma[:, :], T.mb[:, :], Op.mult)
-    run("V", [g_j8], v.tensor_scalar, T.s2[:, :], T.j8[:, :], 8.0, None, Op.is_lt)
-    t_s24 = run("V", [], v.tensor_scalar, T.s4[:, :], T.j8[:, :], 8.0, None, Op.is_ge)
-    t4 = run("V", [t3], v.tensor_tensor, T.f8[:, :], T.bm[:, :], T.j8[:, :], Op.mult)
-    for y in range(8):
-        t_lfm = run("V", [t4], v.tensor_scalar, T.lfm[:, 128 * y:128 * y + 128], T.f8[:, :], float(y + 1), 2.0, Op.is_equal, Op.mult)
-    run("G", [t_s24], g.affine_select, T.smf[:, :], T.s2[:, :], [[-1, 128]], Op.is_equal, 0.0, -1, 1)
-    g_sh = run("G", [], g.affine_select, T.swf[:, :], T.s4[:, :], [[-1, 128]], Op.is_equal, 0.0, 7, 1)
-    g_id = run("G", [t_ones], g.affine_select, T.idm[:, :], T.feat[:, 0:128], [[-1, 128]], Op.is_equal, 0.0, 0, 1)
-    run("S", [t_ones], s.activation, T.c8[:, 0:32], T.feat[:, 0:32], Fn.Copy, scale=0.46875)
-    run("S", [], s.activation, T.c8[:, 32:64], T.feat[:, 0:32], Fn.Copy, scale=-0.03125)
-    run("S", [g_sh], s.activation, T.smb[:, :], T.smf[:, :], Fn.Copy)
-    t_sh = run("S", [], s.activation, T.swb[:, :], T.swf[:, :], Fn.Copy)
-    t_neg = run("S", [g_id], s.activation, T.neg[:, :], T.idm[:, :], Fn.Copy, scale=-1.0)
+    ts([], T.li[:, 1:2], T.lp[:, :], 7, None, Op.bitwise_and)
+    ts([], T.li[:, 2:3], T.lp[:, :], 3, 1, Op.arith_shift_right, Op.bitwise_and)
+    t = ts([], T.li[:, 3:4], T.lp[:, :], 3, None, Op.bitwise_and)
+    t = run("V", [t], v.tensor_copy, T.lf[:, 0:4], T.li[:, 0:4])
+    t_x16 = ts([t], lf["x16"], lf["lane"], 0.0625, None, Op.mult)
+    t_wb = tt([s_wx, g_bm], T.wb[:, :], T.wx[:, :], T.bm[:, :], Op.mult)
+    for j in range(4):
+        g_wj = pick([t_wb], mat(T.wj, j), T.wb[:, :], [[0, 8], [1, 4], [0, 4]], Op.is_equal, 0.0, -j, 0)
+    ts([], lf["ym4"], lf["y"], -1.0, -4.0, Op.mult, Op.add)
+    ts([], lf["u1"], lf["u"], -1.0, 1.0, Op.mult, Op.add)
+    ts([], lf["bu"], lf["u"], -BIG, None, Op.mult)
+    ts([], lf["bu1"], lf["u"], BIG, -BIG, Op.mult, Op.add)
+    ts([], lf["tc"], lf["i"], 128.0, -528.0, Op.mult, Op.add)
+    ts([], lf["d0"], lf["i"], 3.0, 512.0, Op.is_equal, Op.mult)
+    ts([], lf["top"], lf["lane"], 15.0, -512.0, Op.is_equal, Op.mult)
+    t_oh = ts([g_m16], T.oh[:, :], T.m16[:, 0:8], -1.0, lf["lane"], Op.add, Op.is_equal)
+    t = ts([t_oh], lf["d"], lf["d0"], lf["top"], -128.0, Op.add, Op.add)
+    t_d8 = ts([t], lf["d8"], lf["d"], 8.0, None, Op.mult)
+    s_g1 = act([g_gm], T.g1[:, 0:127], T.gm[:, 1:128], Fn.Copy, scale=-1.0)
+    t = run("V", [s_g1], v.memset, T.g1[:, 15::16], 0.0)
+    t_nm = tt([t], T.nm[:, :], T.gm[:, :], T.g1[:, :], Op.add)
+    for q in range(8):
+        s_xq = act([t_oh, g_bm], mat(T.xq, q), T.bm[:, :], Fn.Copy, scale=T.oh[:, q:q + 1])
+    s_neg = act([g_id], T.neg[:, :], T.idm[:, :], Fn.Copy, scale=-1.0)
 
     for k in range(8):
         j, y = k // 2, k % 2
         t = run("V", [ld[k]], v.tensor_copy, T.half[:, :, 32 * j + 16 * y:32 * j + 16 * y + 16], T.raw[:, 8 * k:8 * k + 8, :])
+    s_pw = []
     for i in range(8):
         t_let = run("V", [t], v.transpose, T.let[:, i::8], T.half[:, i, :])
-    t_key = run("V", [t_let, t_lane], v.tensor_scalar, T.keyw[:, B * rank:B * rank + B], T.let[:, :], T.lf[:, 0:1], None, Op.add)
-    send([t_key], T.keyw[:, B * rank:B * rank + B], "hk", hid, hmask, hwidth)
-    run("G", [], g.affine_select, T.xq[:, 0:1024], T.feat[:, 0:1024], [[-1, 8], [-16, 8], [0, 16]], Op.is_equal, 0.0, 0, 1)
-    g_xq = run("G", [], g.affine_select, T.xq[:, 1024:2048], T.feat[:, 0:1024], [[-1, 8], [-16, 8], [0, 16]], Op.is_equal, 0.0, -8, 1)
+        s_pw.append(act([t_let], mat(T.pw, i), T.let[:, i::8], Fn.Exp, scale=math.log(32.0)))
+    own_keys = T.keyw[:, B * rank:B * rank + B]
+    t_key = ts([t_let, t_x16], own_keys, T.let[:, :], lf["x16"], None, Op.add)
+    t_dup = [dma("Y", [t_key], "dup", T.keyw[:, STR + B * rank:STR + B * rank + B], own_keys)]
+    send([t_key], own_keys[:, 0:KD], own_keys[:, 0:KD], "kin%d" % rank)
+    leave([], 0, "hk")
+    act([t_d8], T.no[:, :], T.onef[:, :], Fn.Copy, scale=lf["d8"])
+    t = act([], T.ck[:, :], T.ones[:, 0:512], Fn.Copy, scale=lf["d"])
+    t_ck = act([t], T.ck[:, 0::8], T.ones[:, 0:64], Fn.Copy, scale=lf["tc"])
+    act([], T.b16[:, :], T.bm[:, :], Fn.Copy, scale=0.0625)
+    s_b32 = act([], T.b32[:, :], T.bm[:, :], Fn.Copy, scale=0.03125)
+    t_zt = [act([], T.zt[:, ZW * k:ZW * k + ZW], T.ones[:, :], Fn.Copy, scale=lf["bu" if k % 2 else "bu1"]) for k in range(6)]
+    for u in range(2):
+        g_wu = pick([], mat(T.wu, u), one, [[-16, 8], [0, 2], [-1, 8]], Op.is_equal, 0.0, -8 * u, 1)
+    t = pick([], T.t3[:, :], T.onef[:, :], [[-16, 8], [0, 16]], Op.is_ge, 0.0, 0, 1)
+    pick([t], T.lt[:, :], T.t3[:, :], [[1, 128]], Op.is_gt, 0.0, 0, -1)
+    g_le = pick([], T.le[:, :], T.t3[:, :], [[1, 128]], Op.is_ge, 0.0, 0, -1)
+    g_swp = pick([], T.swp[:, :], one, [[-16, 8], [8, 2], [-1, 8]], Op.is_equal, 0.0, -8, 1)
 
-    t_f = {0: t_ones}
-    for c in list(range(8, 16)) + list(range(1, 8)):
-        t_f[c] = run("V", [], v.tensor_scalar, T.feat[:, B * c:B * c + B], T.let[:, :], float(c), None, Op.is_ge)
-    t_b, t_s, t_ini, t_v = {}, {}, {}, {}
-
-    def count(chi):
-        for c in range(8 * chi, 8 * chi + 8):
-            for h in range(2):
-                at = B * chi + 512 * h
-                t = run("P", [t_f[c], t_lfm], pe.matmul, T.pa[:, at:at + 512], T.lfm[:, 128 * (c % 8):128 * (c % 8) + 128],
-                        T.feat[:, B * c + 512 * h:B * c + 512 * h + 512], c % 8 == 0, c % 8 == 7)
-        return t
-
-    def own(chi):
-        return 4 * (R * chi + rank)
-
-    def shifted(chi, deps):
-        for h in range(2):
-            out = T.pb[:, B * chi + 512 * h:B * chi + 512 * h + 512]
-            t_b[chi] = run("P", t_s[chi] + [t_sh] + deps, pe.matmul, out, T.smb[:, :],
-                           T.sums[:, ASW * chi + 512 * h:ASW * chi + 512 * h + 512], True, chi == 1)
-            if chi == 0:
-                t_b[chi] = run("P", [], pe.matmul, out, T.swb[:, :], T.sums[:, ASW + 512 * h:ASW + 512 * h + 512], False, True)
-
-    def begin(chi, bank, deps):
-        col, lo, mid, hi = 4 * chi, 4 * R * chi, own(chi), 4 * R * (chi + 1)
-        need("V", [("tin%d" % chi, t_in), t_rr] + t_s[chi])
-        if rank:
-            run("V", [], v.tensor_reduce, T.rr[:, col:col + 1], T.tot[:, lo:mid], AxisListType.X, Op.add)
-        t_t = run("V", [], v.tensor_reduce, T.rr[:, col + 1:col + 2], T.tot[:, lo:hi], AxisListType.X, Op.add)
-        t = run("V", [], v.tensor_reduce, T.init[:, col:col + 1], T.tot[:, mid:hi], AxisListType.X, Op.add, negate=True)
-        pt = T.pb[:, 512 * bank:512 * bank + 2]
-        t_pt = run("P", [t_t, t_sh, g_sh] + deps, pe.matmul, pt, T.smf[:, :], T.rr[:, col:col + 2], True, chi == 1)
-        if chi == 0:
-            t_pt = run("P", [], pe.matmul, pt, T.swf[:, :], T.rr[:, 4:6], False, True)
-        t = run("V", [t], v.tensor_scalar, T.init[:, col + 1:col + 2], T.init[:, col:col + 1], float(2 * (16 * NB - 16)), None, Op.add)
-        t_ini[chi] = run("V", [t, t_pt], v.tensor_tensor, T.init[:, col + 2:col + 3], T.init[:, col + 1:col + 2], pt[:, 0:1], Op.subtract)
-        t_v[chi] = run("V", [], v.tensor_scalar, T.wv[:, chi:chi + 1], pt[:, 1:2], -1.0, float(2 * 16 * NB), Op.mult, Op.add)
-
-    def table(chi):
-        t_sc, start, t_hd = t_ini[chi], T.init[:, 4 * chi + 2:4 * chi + 3], []
-        for h in range(2):
-            at, sc = B * chi + 512 * h, ASW * chi + 1 + 512 * h
-            t_sc = run("V", [t_sc, t_b[chi]] + t_s[chi], v.tensor_tensor_scan, T.pa[:, at:at + 512], T.sums[:, sc:sc + 512],
-                       T.pb[:, at:at + 512], start, Op.add, Op.subtract)
-            if h == 0:
-                start = T.init[:, 4 * chi + 3:4 * chi + 4]
-                t_sc = run("V", [t_sc], v.tensor_copy, start, T.pa[:, at + 511:at + 512])
-            t_hd.append(run("S", [t_sc, t_lane], s.activation, T.hd[:, at:at + 512], T.pa[:, at:at + 512], Fn.Copy, scale=T.lf[:, 2:3]))
-        for h, (a, e) in enumerate([(0, HC), (HC, B)]):
-            at, to = B * chi, STR * chi + B * rank
-            t = run("V", [t_hd[h]], v.tensor_tensor, T.base[:, to + a:to + e], T.pa[:, at + a:at + e], T.hd[:, at + a:at + e], Op.subtract)
-            if h == 0:
-                send([t], T.base[:, to + a:to + e], "hb%d" % chi, hid, hmask, hwidth)
-            else:
-                send([t], T.base[:, to + a:to + e], "bin%d" % chi)
-        return t
-
-    def total_of(chi):
-        return T.tot[:, own(chi):own(chi) + 1]
-
-    t = count(1)
-    t_s[1] = [run("S", [t, t_ones, t_rr], s.activation, T.sums[:, ASW + 1:ASW + 1 + B], T.pa[:, B:2 * B], Fn.Copy, accum_out=total_of(1))]
-    send(t_s[1], T.tot[:, own(1):own(1) + 4], "tin1")
-    t = count(0)
-    t_s0 = run("S", [t], s.activation, T.sums[:, 1:513], T.pa[:, 0:512], Fn.Copy, accum_out=total_of(0))
-    t_s1 = run("V", [t], v.tensor_reduce, T.tot[:, own(0) + 1:own(0) + 2], T.pa[:, 512:1024], AxisListType.X, Op.add)
-    send([t_s0, t_s1], T.tot[:, own(0):own(0) + 4], "tin0")
-    t_s[0] = [t_s0, run("V", [], v.tensor_copy, T.sums[:, 513:1025], T.pa[:, 512:1024])]
-    shifted(1, [])
-    begin(1, 0, [])
-    table(1)
-    shifted(0, [t_v[1]])
-    begin(0, 2, [t_v[1], t_b[1]])
-    t_tab = table(0)
-
-    run("V", [], v.memset, T.keyw[:, NB:STR], 1024.0)
-    run("V", [], v.memset, T.base[:, NB:STR], 0.0)
-    t_pad = run("V", [], v.memset, T.base[:, STR + NB:W], 0.0)
-    t = run("V", [t_v[0]], v.tensor_scalar, T.wd[:, :], T.wv[:, :], T.lf[:, 2:3], None, Op.mult)
-    run("V", [lpat], v.tensor_scalar, T.pi[:, :, :], T.pat[:, :, :], 7, None, Op.bitwise_and)
-    t_ci = run("V", [], v.tensor_scalar, T.chi[:, :, :], T.pat[:, :, :], 3, None, Op.arith_shift_right)
-    t_end = run("V", [t, t_pad], v.tensor_tensor, T.base[:, NB:W:STR], T.wv[:, :], T.wd[:, :], Op.subtract)
-    t_cl = run("V", [t_ci], v.tensor_copy, T.cl[:, :, :], T.pi[:, :, :])
+    t_d = []
     for h in range(2):
-        t_ch = run("V", [], v.tensor_scalar, T.ch2[:, :, 32 * h:32 * h + 32], T.chi[:, :, :], float(STR), None, Op.mult)
-    t_c, t_m = {}, {}
-    for st in range(8):
-        bank = st % 4
-        deps = [t_cl, g_xq, t_tab] + ([t_c[st - 4]] if st >= 4 else [])
-        for q in range(16):
-            lo = 512 * bank + q
-            t = run("P", deps, pe.matmul, T.pa[:, lo:512 * bank + 512:16], T.xq[:, 128 * q:128 * q + 128], T.cl[:, st, :], True, True)
-        t_c[st] = run("S", [t], s.activation, T.clx[:, 512 * st:512 * st + 512], T.pa[:, 512 * bank:512 * bank + 512], Fn.Copy)
-        if st == 3:
-            for q in range(16):
-                t = run("P", [g_id], pe.matmul, T.pb[:, 128 * q:128 * q + 128], T.xq[:, 128 * q:128 * q + 128], T.idm[:, :], True, True)
-            for i in range(4):
-                t_eq = run("S", [t], s.activation, T.eq[:, 512 * i:512 * i + 512], T.pb[:, 512 * i:512 * i + 512], Fn.Copy, scale=0.03125)
-    t = run("V", [lst], v.tensor_scalar, T.sf[:, 0, :], T.sti[:, :], 0.0625, -0.03125, Op.mult, Op.add)
-    t = run("V", [t, t_ch], v.tensor_tensor, T.sf[:, 1, :], T.sf[:, 0, :], T.ch2[:, 0, :], Op.add)
-    t_of = run("V", [t], v.tensor_scalar, T.of0[:, :], T.sf[:, 1, :], -0.4375, None, Op.add)
-    t = run("V", [], v.tensor_scalar, T.oi[:, :], T.sf[:, 1, :], -0.4375, None, Op.add)
-    t_kl = run("V", [t], v.tensor_tensor, T.kl[:, 0, :], T.sf[:, 1, :], T.oi[:, :], Op.subtract)
-    for st in range(8):
-        t_m[st] = run("V", [t_c[st], t_lane], v.tensor_scalar, T.msk[:, 512 * st:512 * st + 512], T.clx[:, 512 * st:512 * st + 512],
-                      T.lf[:, 1:2], None, Op.is_equal)
-        if st == 3:
-            t_dup = run("V", [("kin", k_in), t_pad], v.tensor_scalar, T.keyw[:, STR:W], T.keyw[:, 0:STR], -8.0, None, Op.add)
+        for j in range(4):
+            f = T.feat[:, B * j + 512 * h:B * j + 512 * h + 512]
+            t = ts([s_pw[4 * h + 3]], f, T.pw[:, 512 * h:512 * h + 512], 32.0 ** (4 * j - 1), 32.0 ** (4 * j + 3), Op.max, Op.min)
+            t = mm([t, g_wj], bank(h), mat(T.wj, j), f, j == 0, j == 3)
+        t_d.append(t)
+    t_nn = []
+    for h in range(2):
+        cols = slice(512 * h, 512 * h + 512)
+        t = ts([t_d[h]], T.hq[:, cols], bank(h), -4.0, None, Op.add)
+        t_nn.append(tt([t], T.nn[:, cols], bank(h), T.hq[:, cols], Op.subtract))
+        for i in range(4 * h, 4 * h + 4):
+            t_sb = mm([t_nn[h], t_nm], bank(2)[:, 0:128], T.nm[:, :], mat(T.nn, i), i == 0, i == 7)
+        if h == 0:
+            run("V", [], v.memset, T.vr[:, 0:1], 0.0)
+            run("V", [], v.memset, T.vr[:, 129:132], 0.0)
+    t_cl = run("V", [lpat], v.tensor_copy, T.cl[:, :], T.pat[:, :])
+    t_vr = run("V", [t_sb, t_ck], v.tensor_tensor_scan, T.vr[:, 1:129], T.no[:, :], bank(2)[:, 0:128], 0.0, Op.add, Op.add)
+    mine = T.tot[:, 4 * rank:4 * rank + 4]
+    send([t_vr], T.vr[:, 128:132], mine, "tin")
+    t_tot = run("V", [t_vr], v.tensor_copy, mine, T.vr[:, 128:132])
 
-    of = [T.of0, T.of1]
-    pend = [("bin1", b_in), ("bin0", b_in), t_end]
-    ps = [T.pa[:, 1024:1088], T.pa[:, 1536:1600]]
-    free = [t_c[7], t_eq, t_ch, t_neg]
-    for st in range(8):
-        o, P = of[st % 2], ps[st % 2]
-        for h in range(2):
-            run("P", free, pe.matmul, T.pa[:, 512 * h:512 * h + 512], T.idm[:, :], T.clx[:, 512 * st:512 * st + 512], True, False)
-        run("P", [], pe.matmul, P, T.idm[:, :], T.c8[:, :], True, False)
-        if st < 7:
-            run("P", [], pe.matmul, P, T.idm[:, :], T.ch2[:, st + 1, :], False, False)
-        t_kg, t_y, t_ym = [], [], []
-        for h in range(2):
-            t_kg.append(run("S", [t_of, t_dup], s.activation, T.kg[:, 512 * h:512 * h + 512],
-                            T.keyw[:, 0:W].indirect(o[:, 32 * h:32 * h + 32]), Fn.Copy))
-            t_ym.append(run("V", [t_of, t_m[st]] + pend, v.tensor_tensor, T.ym[:, 512 * h:512 * h + 512],
-                            T.base[:, 0:W].indirect(o[:, 32 * h:32 * h + 32]), T.msk[:, 512 * st:512 * st + 512], Op.mult))
-        for h in range(2):
-            for q in range(16):
-                run("P", [t_kl], pe.matmul, T.pa[:, 512 * h + q:512 * h + 512:16], T.xq[:, 128 * q:128 * q + 128],
-                    T.kl[:, st % 2, 32 * h:32 * h + 32], False, False)
-            t_y.append(run("P", [t_kg[h]], pe.matmul, T.pa[:, 512 * h:512 * h + 512], T.neg[:, :], T.kg[:, 512 * h:512 * h + 512], False, True))
-        t_xa = run("S", [t_y[0]], s.activation, T.xs[:, 0:512], T.pa[:, 0:512], Fn.Sign)
-        t_xb = run("V", [t_y[1]], v.tensor_scalar, T.xs[:, 512:1024], T.pa[:, 512:1024], 0.0, 2.0, Op.is_gt, Op.mult)
-        for q in range(16):
-            run("P", [t_ym[1]], pe.matmul, P, T.eq[:, 128 * q:128 * q + 128], T.ym[:, q::16], False, False)
-        for q in range(16):
-            t_p = run("P", [t_xa, t_xb], pe.matmul, P, T.eq[:, 128 * q:128 * q + 128], T.xs[:, q::16], False, q == 15)
-        free = []
-        if st < 7:
-            t_of = run("V", [t_p], v.tensor_scalar, of[1 - st % 2][:, :], P, -0.4375, None, Op.add)
-            t = run("V", [], v.tensor_scalar, T.oi[:, :], P, -0.4375, None, Op.add)
-            t_kl = run("V", [t], v.tensor_tensor, T.kl[:, 1 - st % 2, :], P, T.oi[:, :], Op.subtract)
+    for u in range(2):
+        t = mm([t_cl, g_wu], bank(7)[:, u::2], mat(T.wu, u), T.cl[:, :], True, True)
+    s_cd = act([t], T.cd[:, :], bank(7), Fn.Copy)
+    s_nsw = act([g_swp], T.nsw[:, :], T.swp[:, :], Fn.Copy, scale=-1.0)
+    s_ab = []
+
+    def letters(st):
+        for q in range(8):
+            t = mm([s_cd, s_xq, t_nn[1]] + s_ab[st - 2:st - 1], bank(st % 2)[:, q::8], mat(T.xq, q), T.cd[:, 64 * st:64 * st + 64], True, True)
+        s_ab.append(act([t], T.ab[:, 512 * st:512 * st + 512], bank(st % 2), Fn.Abs, bias=lf["ym4"]))
+
+    for h in range(2):
+        e = bank(4 + h)
+        mm([t_ck, g_id], e, T.idm[:, :], T.ck[:, :], True, False)
+        for i in range(8):
+            mm([t_nn[1]], e[:, i::8], T.gm[:, :], mat(T.nn, i)[:, 64 * h:64 * h + 64], False, False)
+            if i:
+                mm([], e[:, i::8], T.g1[:, :], mat(T.nn, i - 1)[:, 64 * h:64 * h + 64], False, False)
+    for st in range(EARLY):
+        letters(st)
+    own = SW * rank
+    t = run("V", [], v.memset, T.zr[:, :], 1.0)
+    run("V", [], v.memset, T.ship[:, own + PARTS[1][2]:own + PARTS[1][3]], 0.0)
+    t_pad = run("V", [], v.memset, T.ship[:, own + SW - 8:own + SW], 0.0)
+    t_zr = run("V", [t], v.memset, T.zr[:, 0::8], 0.0)
+    t_z = run("V", [], v.memset, T.zs[:, :], -4 * SEL)
+    ts([], lf["sl"], lf["u"], SEL, -SEL, Op.mult, Op.add)
+    ts([], lf["zs"], lf["u"], -5 * SEL, SEL, Op.mult, Op.add)
+    for x in range(2):
+        mine = [p for p in SHARE[x] if p[0] == "V"]
+        a, k = mine[0][1:] if mine else (1, 1)
+        t = ts([], T.li[:, 4 + x:5 + x], T.lp[:, :], k - 1, None, Op.bitwise_and)
+        t_k = ts([t], T.kap[:, x:x + 1], T.li[:, 4 + x:5 + x], float(a), 0.5, Op.not_equal, Op.mult)
+    ts([lst], T.s1[:, :], T.sti[:, :], 15, None, Op.bitwise_and)
+    ts([t_k], T.kap[:, 2:4], T.kap[:, 0:2], -1.0, 0.46875, Op.mult, Op.add)
+    ts([], T.kap[:, 4:6], T.kap[:, 0:2], -1.0, None, Op.mult)
+    t = ts([], T.kap[:, 6:8], T.kap[:, 0:2], lf["sl"], None, Op.add)
+    t_zs = ts([t_z], T.zs[:, 1::2], T.onef[:, 0:32], lf["zs"], None, Op.mult)
+    t_kap = ts([t], T.kap[:, 8:10], T.kap[:, 6:8], -0.46875, None, Op.add)
+    kap = {n: [T.kap[:, 2 * k + x:2 * k + x + 1] for x in range(2)] for k, n in enumerate(["k", "c", "n", "y", "o"])}
+    ts([], T.s2[:, :], T.sti[:, :], 4, None, Op.arith_shift_right)
+    t = ts([], T.s3[:, :], T.pat[:, 0:32], 8.0, float(STR), Op.is_ge, Op.mult)
+    t_kc = ts([], T.kc[:, :], T.s1[:, :], 0.0625, None, Op.mult)
+    for x in range(2):
+        t2 = tt([t], T.s4[:, 32 * x:32 * x + 32], T.s2[:, 32 * x:32 * x + 32], T.s3[:, :], Op.add)
+    run("V", [], v.memset, T.keyw[:, NB:STR], 1024.0)
+    run("V", [], v.memset, T.keyw[:, STR + NB:W], 1024.0)
+    t = run("V", [t2], v.tensor_copy, T.off[:, 0:64], T.s4[:, :])
+    run("V", [], v.memset, T.base[:, NB + 1:STR], 0.0)
+    t_fill = run("V", [], v.memset, T.base[:, STR + NB + 1:W], 0.0)
+    t_ch = ts([s_cd], T.ch[:, :], T.cd[:, :], 8.0, float(STR), Op.is_ge, Op.mult)
+    t_of, t_kl, t_m = [t, t], [], []
+
+    def masks(st):
+        t_m.append(ts([s_ab[st]], T.msk[:, 512 * st:512 * st + 512], T.ab[:, 512 * st:512 * st + 512], 4.0, 2.0, Op.is_equal, Op.mult))
+
+    for st in range(MASKS):
+        masks(st)
+
+    cols = T.tot[:, 0:4 * R:4]
+    if rank:
+        mm([("tin", width * (R - 1)), t_tot, g_le], bank(3)[:, 0:rank], T.le[:, :], cols[:, 0:rank], True, True)
+    t = mm([("tin", width * (R - 1)), t_tot, g_le], bank(3)[:, rank:R], T.lt[:, :], cols[:, rank:R], True, True)
+    t = run("V", [t], v.tensor_reduce, T.init[:, :], bank(3)[:, 0:R], AxisListType.X, Op.add)
+    val = bank(2)[:, 256:385]
+    t_hb = ts([t], T.hb[:, 1:130], T.vr[:, 0:129], T.init[:, :], 256.0, Op.add, Op.max)
+    t = ts([], val, T.vr[:, 0:129], T.init[:, :], None, Op.add)
+    t_rb = tt([t], T.rb[:, 0:129], val, T.hb[:, 1:130], Op.subtract)
+    t_e2 = [mm([t_rb], bank(4 + h)[:, 0::8], T.idm[:, :], T.rb[:, 64 * h:64 * h + 64], False, True) for h in range(2)]
+    s_dh = []
+    for b0, n, at, low, end in PARTS:
+        a, k = b0 // 8, (n + 7) // 8
+        out = bank(6)[:, a:a + k]
+        mm([t_hb, s_nsw], out, T.swp[:, :], T.hb[:, 1 + a:1 + a + k], True, False)
+        t = mm([], out[:, 1:], T.nsw[:, :], T.hb[:, 1 + a:a + k], False, True)
+    for b0, n, at, low, end in PARTS:
+        a, k = b0 // 8, (n + 7) // 8
+        s_dh.append(act([t, t_pad], T.ship[:, own + at:own + at + k], bank(6)[:, a:a + k], Fn.Copy))
+    lo_a, lo_b = own + PARTS[0][3], own + PARTS[1][3]
+    scan = v.tensor_tensor_scan
+    t_la = run("V", [t_e2[0], t_zr], scan, T.ship[:, lo_a:lo_a + HC], T.zr[:, 0:HC], bank(4)[:, 0:HC], 0.0, Op.mult, Op.add)
+    leave([t_la, s_dh[0]], 1, "hl")
+    if HC < 512:
+        run("V", [], scan, T.ship[:, lo_b:lo_b + 512 - HC], T.zr[:, 0:512 - HC], bank(4)[:, HC:512], 0.0, Op.mult, Op.add)
+    run("V", [t_pad], v.tensor_copy, T.ship[:, lo_b + B - HC:lo_b + B - HC + 1], T.rb[:, 128:129])
+    t_lb = run("V", [t_e2[1]], scan, T.ship[:, lo_b + 512 - HC:lo_b + B - HC], T.zr[:, :], bank(5), 0.0, Op.mult, Op.add)
+    part_b = T.ship[:, own + PARTS[1][2]:own + SW]
+    send([t_lb, s_dh[1]], part_b, part_b, "lb%d" % rank)
+
+    used = {}
+
+    def unfold(r, part, slot, deps):
+        b0, n, at, low, end = PARTS[part]
+        n -= part == 1 and r < R - 1
+        k = (n + 7) // 8
+        for chi in range(2):
+            z = T.zt[:, ZW * (2 * slot + chi):ZW * (2 * slot + chi) + n]
+            t = act(deps + [t_zt[2 * slot + chi]] + used.get((slot, chi), []), z[:, 0::8], T.ship[:, SW * r + at:SW * r + at + k], Fn.Identity,
+                    scale=lf["u1" if chi else "u"], bias=lf["bu" if chi else "bu1"])
+            to = STR * chi + B * r + b0
+            t = run("V", deps + [t], scan, T.base[:, to:to + n], z, T.ship[:, SW * r + low:SW * r + low + n], 0.0, Op.add, Op.max)
+            used[slot, chi] = [t]
+        return t
+
+    for q in range(8):
+        t_e = pick([s_b32], mat(T.e32, q), T.b32[:, :], [[0, 16], [1, 8]], Op.is_equal, 0.0, -q, 0)
+    for q in range(8):
+        if any(e == "V" and q % k == a for x in range(2) for e, a, k in SHARE[x]):
+            t_e = pick([], mat(T.e16, q), T.b16[:, :], [[0, 16], [1, 8]], Op.is_equal, 0.0, -q, 0)
+    unfold(rank, 0, 0, [t_la, s_dh[0]])
+    unfold(rank, 1, 1, [t_lb, s_dh[1]])
+    for st in range(EARLY, 8):
+        letters(st)
+    for x in range(2):
+        for u in range(2):
+            out = bank(7)[:, 64 * x + u:64 * x + 64:2]
+            mm([t_kc, s_cd], out, mat(T.wu, u), T.kc[:, 32 * x:32 * x + 32], True, False)
+            t = mm([], out, mat(T.wu, u), T.cl[:, 0:32], False, True)
+    for x in range(2):
+        t_kl.append(act([t, t_kap], T.kl[:, 64 * x:64 * x + 64], bank(7)[:, 64 * x:64 * x + 64], Fn.Identity, bias=kap["n"][x]))
+    for st in range(MASKS, 8):
+        masks(st)
+    ring = [(rank + k) % R for k in range(1, R)]
+    for r, q in zip(ring, DUP):
+        deps = [("kin%d" % r, width + hw)]
+        to, src = T.keyw[:, STR + B * r:STR + B * r + B], T.keyw[:, B * r:B * r + B]
+        if q == "V":
+            t_dup.append(run("V", deps, v.tensor_copy, to, src))
+        elif q == "S":
+            t_dup.append(act(deps, to, src, Fn.Copy))
         else:
-            t = run("V", [t_p], v.tensor_scalar, T.yo[:, :], P, 16.0, 0.5, Op.mult, Op.add)
-            dma("Y", [t], "out", T.y[:, :], T.yo[:, :])
+            t_dup.append(dma("Y", deps, "dup", to, src))
+    t_dup = [t if t[0] != "dup" else ("dup", total["dup"]) for t in t_dup]
+    for part, sem, n in [(1, "lb", width), (0, "la", hw)]:
+        for slot, r in enumerate(ring):
+            t_base = unfold(r, part, slot, [("%s%d" % (sem, r), n)])
+        if part:
+            for x in range(2):
+                s_clb = act([t_kap, s_cd], T.clb[:, 512 * x + 64:512 * x + 512], T.cd[:, 64:512], Fn.Identity, bias=kap["c"][x])
 
-    for sem in ["cV", "cS", "cP", "cG", "out", "snt"]:
+    P = [bank(6)[:, 0:64], bank(7)[:, 0:64]]
+    banks = [{"V": bank(0), "S": bank(1)}, {"V": bank(2), "S": bank(3)}]
+    lay = []
+    for x in range(2):
+        at, d, parts = {"V": 0, "S": 0}, {}, []
+        for e, a, k in SHARE[x]:
+            n = 512 // k
+            parts.append((e, a, k, at[e], n))
+            for q in range(a, 8, k):
+                d[q] = (e, slice(at[e] + q // k, at[e] + n, 8 // k))
+            at[e] += n
+        lay.append((d, parts, at))
+    xs = [{"V": T.xs[:, 512 * x:512 * x + 512], "S": T.xs[:, 512 * x + lay[x][2]["V"]:512 * x + 512]} for x in range(2)]
+    kg = [T.kg[:, 512 * x:512 * x + 512] for x in range(2)]
+    ym = [T.ym[:, 512 * x:512 * x + 512] for x in range(2)]
+    tk = [{}, {}]
+
+    def offs(x, st):
+        at = 64 * (st % 2) + 32 * x
+        return T.off[:, at:at + 32]
+
+    def keys(x, st):
+        tk[x]["kg"] = act([t_of[x], t_fill] + t_dup, kg[x], T.keyw[:, 0:W].indirect(offs(x, st)), Fn.Copy)
+
+    def bases(x, st, a, e):
+        tk[x]["ym"] = tt([t_of[x], t_m[st], t_base], ym[x][:, 16 * a:16 * e], T.base[:, 0:W].indirect(offs(x, st)[:, a:e]),
+                         T.msk[:, 512 * st + 16 * a:512 * st + 16 * e], Op.mult)
+
+    def spread(x, st, deps=()):
+        begun = set()
+        for q in range(8):
+            e, c = lay[x][0][q]
+            alone = e == "V"
+            tk[x]["sp"] = mm([t_kl[x]] + list(deps), banks[x][e][:, c], mat(T.xq, q), T.kl[:, 64 * x:64 * x + 64], alone or e not in begun, alone)
+            begun.add(e)
+        if st < 7:
+            mm([t_ch], P[x], T.idm[:, :], T.ch[:, 64 * st + 64:64 * st + 128], True, False)
+
+    def minus(x):
+        mine = [p for p in lay[x][1] if p[0] == "S"]
+        for e, a, k, at, n in mine:
+            tk[x]["ng"] = mm([tk[x]["kg"], s_neg], banks[x]["S"][:, at:at + n], T.neg[:, :], kg[x][:, a::k], False, at == mine[-1][3])
+
+    def compare(x, e):
+        if e == "S":
+            n = lay[x][2]["S"]
+            tk[x]["S"] = act([tk[x]["ng"]], xs[x]["S"][:, 0:n], banks[x]["S"][:, 0:n], Fn.Sign, bias=0.46875)
+        for e2, a, k, at, n in lay[x][1]:
+            if e == e2 == "V":
+                tk[x]["V"] = tt([tk[x]["kg"], tk[x]["sp"]], xs[x]["V"][:, at:at + n], kg[x][:, a::k], banks[x]["V"][:, at:at + n], Op.is_lt)
+
+    def sum_bases(x, st):
+        for q in range(8):
+            mm([tk[x]["ym"], t_e], P[x], mat(T.e32, q), ym[x][:, q::8], st == 7 and q == 0, False)
+
+    def sum_signs(x, e):
+        qs = [q for q in range(8) if lay[x][0][q][0] == e]
+        for q in qs:
+            tk[x]["P"] = mm([tk[x][e]], P[x], mat(T.e32 if e == "S" else T.e16, q), xs[x][e][:, lay[x][0][q][1]], False, e == "S" and q == qs[-1])
+
+    def choose(x, st):
+        sel, oi = T.sel[:, 64 * x:64 * x + 64], T.oi[:, 64 * x:64 * x + 64]
+        t = run("V", [tk[x]["P"], t_zs], scan, sel, T.zs[:, :], P[x], 0.0, Op.add, Op.max)
+        if st < 7:
+            t2 = tt([s_clb], oi, P[x], T.clb[:, 512 * x + 64 * st + 64:512 * x + 64 * st + 128], Op.subtract)
+            t_of[x] = ts([t], offs(x, st + 1), sel[:, 1::2], kap["o"][x], None, Op.add)
+            t_kl[x] = tt([t2], T.kl[:, 64 * x:64 * x + 64], P[x], oi, Op.subtract)
+        else:
+            t_of[x] = ts([t], T.yo[:, 32 * x:32 * x + 32], sel[:, 1::2], kap["y"][x], 16.0, Op.add, Op.mult)
+
+    A, Z = 0, 1
+    for st in range(8):
+        keys(A, st)
+        bases(A, st, 0, 16)
+        if st:
+            sum_signs(Z, "S")
+            choose(Z, st - 1)
+        spread(A, st, [] if st else [s_ab[7], t_kl[1], t_lb])
+        minus(A)
+        keys(Z, st)
+        bases(A, st, 16, 32)
+        spread(Z, st)
+        compare(A, "V")
+        sum_bases(A, st)
+        sum_signs(A, "V")
+        minus(Z)
+        compare(A, "S")
+        bases(Z, st, 0, 32)
+        compare(Z, "V")
+        sum_signs(A, "S")
+        compare(Z, "S")
+        sum_bases(Z, st)
+        sum_signs(Z, "V")
+        choose(A, st)
+    sum_signs(Z, "S")
+    choose(Z, 7)
+    dma("Y", t_of, "out", T.y[:, :], T.yo[:, :])
+
+    for sem in ["cV", "cS", "cP", "cG", "out", "snt", "dup"]:
         need("G", [(sem, total[sem])])

@@ -6,23 +6,21 @@ R, B = 4, 1024
 NB = R * B
 STR = 4224
 W = 2 * STR
-KD = 256
 HC = 448
-EARLY, MASKS = 4, 1
-DUP = "YVS"
+EARLY = 1
 BIG = 131072.0
 SEL = 16384.0
 PARTS = [(0, HC, 0, HC // 8, HC // 8 + HC),
          (HC, B + 1 - HC, HC // 8 + HC, HC // 8 + HC + (B - HC) // 8 + 8, HC // 8 + HC + (B - HC) // 8 + B - HC + 16)]
 SW = PARTS[1][4]
 ZW = max(HC, B - HC) + 8
-SHARE = [[("V", 0, 2), ("S", 1, 2)], [("S", 0, 1)]]
+SHARE = [[("V", 0, 2), ("S", 1, 2)], [("V", 0, 2), ("S", 1, 2)]]
 
 bf, f32, i32 = "bfloat16", "float32", "int32"
 SCRATCH = {
     "raw": ("sbuf", [128, 64, 16], i32),
-    "half": ("sbuf", [128, 8, 128], bf),
-    "let": ("sbuf", [128, B], bf),
+    "half": ("sbuf", [128, 16, 64], bf),
+    "let": ("sbuf", [128, 16, 64], bf),
     "pw": ("sbuf", [128, B], bf),
     "feat": ("sbuf", [128, 4 * B], bf),
     "hq": ("sbuf", [128, B], i32),
@@ -30,10 +28,11 @@ SCRATCH = {
     "keyw": ("sbuf", [128, W], bf),
     "base": ("sbuf", [128, W], bf),
     "ship": ("sbuf", [128, R * SW], bf),
-    "zt": ("sbuf", [128, 6 * ZW], bf),
+    "zt": ("sbuf", [128, 4 * ZW], bf),
     "vr": ("sbuf", [128, 132], f32),
     "tot": ("sbuf", [128, 4 * R], f32),
     "init": ("sbuf", [128, 1], f32),
+    "le": ("sbuf", [128, 128], f32),
     "hb": ("sbuf", [128, 130], bf),
     "rb": ("sbuf", [128, 130], bf),
     "ones": ("sbuf", [128, ZW], bf),
@@ -53,12 +52,16 @@ SCRATCH = {
     "b32": ("sbuf", [128, 128], bf),
     "b16": ("sbuf", [128, 128], bf),
     "kap": ("sbuf", [128, 10], f32),
-    "oh": ("sbuf", [128, 8], f32),
+    "oh": ("sbuf", [128, 16], f32),
+    "m8": ("sbuf", [128, 128], bf),
+    "yk": ("sbuf", [128, 128], bf),
+    "n4": ("sbuf", [128, 128], bf),
+    "ih": ("sbuf", [128, 128], bf),
+    "mq": ("sbuf", [128, 8 * 128], bf),
     "gm": ("sbuf", [128, 128], bf),
     "g1": ("sbuf", [128, 128], bf),
     "nm": ("sbuf", [128, 128], bf),
     "lt": ("sbuf", [128, 128], f32),
-    "le": ("sbuf", [128, 128], f32),
     "idm": ("sbuf", [128, 128], bf),
     "neg": ("sbuf", [128, 128], bf),
     "swp": ("sbuf", [128, 128], bf),
@@ -67,16 +70,15 @@ SCRATCH = {
     "xq": ("sbuf", [128, 8 * 128], bf),
     "e16": ("sbuf", [128, 8 * 128], bf),
     "e32": ("sbuf", [128, 8 * 128], bf),
-    "ck": ("sbuf", [128, 512], bf),
+    "fix": ("sbuf", [128, 704], bf),
     "zr": ("sbuf", [128, 512], bf),
     "zs": ("sbuf", [128, 64], f32),
-    "no": ("sbuf", [128, 128], f32),
     "pat": ("sbuf", [128, 256], i32),
     "cl": ("sbuf", [128, 256], bf),
     "cd": ("sbuf", [128, 512], bf),
     "ch": ("sbuf", [128, 512], bf),
-    "clb": ("sbuf", [128, 2 * 512], f32),
-    "ab": ("sbuf", [128, 8 * 512], bf),
+    "sq": ("sbuf", [128, 512], bf),
+    "clb": ("sbuf", [128, 512], f32),
     "msk": ("sbuf", [128, 8 * 512], bf),
     "sti": ("sbuf", [128, 64], i32),
     "s1": ("sbuf", [128, 64], i32),
@@ -95,13 +97,13 @@ SCRATCH = {
     "pa": ("psum", [128, 2048], f32),
     "pb": ("psum", [128, 2048], f32),
 }
-SEMAPHORES = (["cV", "cS", "cP", "cG", "lpat", "lst", "out", "hk", "hl", "tin", "snt", "dup"] + ["ld%d" % k for k in range(8)]
+SEMAPHORES = (["cV", "cS", "cP", "cG", "lpat", "lst", "out", "k0", "k1", "tv", "la", "tin", "snt"] + ["ld%d" % k for k in range(8)]
               + ["%s%d" % (n, r) for n in ("kin", "la", "lb") for r in range(R)])
 
 
 def helpers(rank_core, T, topo):
     return [c for c in topo.cores_of(rank_core)
-            if topo.die(c) != topo.die(rank_core) and all(topo.may_write(c, d) for d in T.cores if d != rank_core)]
+            if c != rank_core and all(topo.may_write(c, d) for d in T.cores if d != rank_core)]
 
 
 def route(core, to, topo):
@@ -113,35 +115,44 @@ def route(core, to, topo):
     return ids, mask, bin(mask).count("1")
 
 
-def halves(mask, n):
+def deal(mask, n):
     bits = [e for e in range(mask.bit_length()) if mask >> e & 1]
     k = len(bits) // n
     return [sum(1 << e for e in bits[k * i:k * i + k]) for i in range(n)]
 
 
-def inside(home, hands, T, topo):
+def ways(rank, T, topo):
+    home = T.cores[rank]
+    hands = helpers(home, T, topo)
+    near = [c for c in hands if topo.die(c) == topo.die(home)]
+    far = [c for c in hands if c not in near]
     away = route(home, [c for c in T.cores if c != home], topo)[1]
-    return halves(route(home, hands, topo)[1] & ~away, len(hands))
+    every = route(home, hands, topo)[1]
+    stay = every & ~away
 
+    def cut(buf, at, n, to, masks):
+        k = n // len(to)
+        return [(buf[:, at + k * i:at + k * i + k], c, m) for i, (c, m) in enumerate(zip(to, masks))]
 
-def relayed(T, rank, i, n):
-    kw, lw = (B - KD) // n, PARTS[0][4] // n
-    ka, la = B * rank + KD + kw * i, SW * rank + lw * i
-    return T.keyw[:, ka:ka + kw], T.ship[:, la:la + lw]
+    return {"k0": ("kin%d" % rank, cut(T.keyw, B * rank, B // 2, far, deal(stay, len(far)))),
+            "k1": ("kin%d" % rank, cut(T.keyw, B * rank + B // 2, B // 2, [None] + near, [away] + deal(stay, len(near)))),
+            "tv": ("tin", cut(T.tot, 4 * rank, 4, [None], [away])),
+            "la": ("la%d" % rank, cut(T.ship, SW * rank, PARTS[0][4], far, deal(every, len(far)))),
+            "lb": ("lb%d" % rank, cut(T.ship, SW * rank + PARTS[0][4], SW - PARTS[0][4], [None], [away]))}
 
 
 def hand_on(g, core, rank, T, topo):
-    home = T.cores[rank]
-    hands = helpers(home, T, topo)
     ids, mask, width = route(core, [T.cores[(rank + k) % R] for k in range(1, R)], topo)
-    came = bin(inside(home, hands, T, topo)[0]).count("1")
-    pieces = relayed(T, rank, hands.index(core), len(hands))
-    for piece, here, there in zip(pieces, ["hk", "hl"], ["kin%d" % rank, "la%d" % rank]):
-        g.wait_ge(T.sem[here], came)
-        g.remote_dma_fused([RemoteDMATransfer(dst_ids=ids, dma_engine_mask=mask, remote_sem=T.sem[there],
-                                              srcs=[piece], dsts=[piece for _ in ids], alu_op=0)],
-                           local_sem=T.sem.snt)
-    g.wait_ge(T.sem.snt, 2 * width)
+    sent = 0
+    for name, (there, parts) in ways(rank, T, topo).items():
+        for piece, hand, came in parts:
+            if hand == core:
+                g.wait_ge(T.sem[name], bin(came).count("1"))
+                g.remote_dma_fused([RemoteDMATransfer(dst_ids=ids, dma_engine_mask=mask, remote_sem=T.sem[there],
+                                                      srcs=[piece], dsts=[piece for _ in ids], alu_op=0)],
+                                   local_sem=T.sem.snt)
+                sent += width
+    g.wait_ge(T.sem.snt, sent)
 
 
 def rank_program(g, core, T, topo):
@@ -197,24 +208,23 @@ def rank_program(g, core, T, topo):
         return (T.pa if k < 4 else T.pb)[:, 512 * (k % 4):512 * (k % 4) + 512]
 
     others = [T.cores[(rank + k) % R] for k in range(1, R)]
-    hands = helpers(core, T, topo)
     ids, mask, width = route(core, others, topo)
-    hids, hmasks = route(core, hands, topo)[0], inside(core, hands, T, topo)
-    hwidth = bin(sum(hmasks)).count("1")
-    hw = len(hands) * route(hands[0], others, topo)[2]
+    calls = ways(rank, T, topo)
 
-    def send(deps, src, dst, sem):
-        need("G", deps)
-        g.remote_dma_fused([RemoteDMATransfer(dst_ids=ids, dma_engine_mask=mask, remote_sem=T.sem[sem],
-                                              srcs=[src], dsts=[dst for _ in ids], alu_op=0)], local_sem=T.sem.snt)
-        total["snt"] = total.get("snt", 0) + width
+    def landed(sem):
+        r = int(sem[-1])
+        return (sem, width * sum(len(parts) for there, parts in ways(r, T, topo).values() if there == sem))
 
-    def leave(deps, which, sem):
+    def leave(deps, name):
         need("G", deps)
-        parts = [relayed(T, rank, i, len(hands))[which] for i in range(len(hands))]
-        g.remote_dma_fused([RemoteDMATransfer(dst_ids=[hids[i]], dma_engine_mask=hmasks[i], remote_sem=T.sem[sem],
-                                              srcs=[p], dsts=[p], alu_op=0) for i, p in enumerate(parts)], local_sem=T.sem.snt)
-        total["snt"] = total.get("snt", 0) + hwidth
+        there, parts = calls[name]
+        moves = []
+        for piece, hand, eng in parts:
+            to = ids if hand is None else route(core, [hand], topo)[0]
+            moves.append(RemoteDMATransfer(dst_ids=to, dma_engine_mask=eng, remote_sem=T.sem[there if hand is None else name],
+                                           srcs=[piece], dsts=[piece for _ in to], alu_op=0))
+            total["snt"] = total.get("snt", 0) + bin(eng).count("1")
+        g.remote_dma_fused(moves, local_sem=T.sem.snt)
 
     ld = []
     for k in range(8):
@@ -229,148 +239,177 @@ def rank_program(g, core, T, topo):
     g_lp = run("G", [], g.iota, T.lp[:, :], [[0, 1]], 0, 1)
     g_m16 = run("G", [], g.iota, T.m16[:, :], [[0, 8], [1, 16]], 1, 0, **fl)
     t_one = run("V", [], v.memset, T.ones[:, :], 1.0)
+    g_m8 = run("G", [], g.iota, T.m8[:, :], [[0, 16], [1, 8]], 0, 0, **fl)
     run("V", [], v.memset, T.onef[:, :], 1.0)
     t_c32 = run("V", [], v.memset, T.c32[:, :], 32.0)
     t = pick([t_one], T.t1[:, :], one, [[-16, 8], [0, 16]], Op.is_ge, 0.0, 0, 1)
     g_bm = pick([t], T.bm[:, :], T.t1[:, :], [[16, 8], [0, 16]], Op.is_ge, 0.0, 15, -1)
-    g_id = pick([], T.idm[:, :], one, [[-1, 128]], Op.is_equal, 0.0, 0, 1)
     t = pick([t_c32], T.t2[:, :], T.c32[:, :], [[-1, 128]], Op.is_ge, 0.0, 0, 1)
-    g_gm = pick([t], T.gm[:, :], T.t2[:, :], [[4, 32], [0, 4]], Op.is_ge, 0.0, 3, -1)
     s_wx = act([g_m16], T.wx[:, :], T.m16[:, :], Fn.Exp, scale=-math.log(32.0))
 
     lf = {n: T.lf[:, k:k + 1] for k, n in enumerate(
-        ["lane", "y", "u", "i", "x16", "ym4", "u1", "bu", "bu1", "tc", "d0", "top", "d", "d8", "sl", "zs"])}
+        ["lane", "y", "u", "odd", "x16", "sb", "sg", "u1", "bu", "bu1", "sl", "zs", "yy", "mb", "kc", "kn", "ky", "ko"])}
+    g_gm = pick([t], T.gm[:, :], T.t2[:, :], [[4, 32], [0, 4]], Op.is_ge, 0.0, 3, -1)
     run("V", [g_lp], v.tensor_scalar, T.li[:, 0:1], T.lp[:, :], 15, None, Op.bitwise_and)
     ts([], T.li[:, 1:2], T.lp[:, :], 7, None, Op.bitwise_and)
     ts([], T.li[:, 2:3], T.lp[:, :], 3, 1, Op.arith_shift_right, Op.bitwise_and)
-    t = ts([], T.li[:, 3:4], T.lp[:, :], 3, None, Op.bitwise_and)
-    t = run("V", [t], v.tensor_copy, T.lf[:, 0:4], T.li[:, 0:4])
-    t_x16 = ts([t], lf["x16"], lf["lane"], 0.0625, None, Op.mult)
-    t_wb = tt([s_wx, g_bm], T.wb[:, :], T.wx[:, :], T.bm[:, :], Op.mult)
+    t = ts([], T.li[:, 3:4], T.lp[:, :], 1, None, Op.bitwise_and)
+    run("V", [], v.memset, T.vr[:, 0:1], 0.0)
+    run("V", [], v.memset, T.vr[:, 129:132], 0.0)
+    t_lf = run("V", [t], v.tensor_copy, T.lf[:, 0:4], T.li[:, 0:4])
+    for name, src, a, b in [("x16", "lane", 0.0625, 0.0), ("sb", "u", -1.0, -3.0), ("sg", "u", -2.0, 1.0), ("u1", "u", -1.0, 1.0), ("bu", "u", -BIG, 0.0),
+                            ("bu1", "u", BIG, -BIG), ("sl", "u", SEL, -SEL), ("zs", "u", -5 * SEL, SEL)]:
+        ts([t_lf], lf[name], lf[src], a, b, Op.mult, Op.add)
+    t_oh = ts([g_m16], T.oh[:, 0:8], T.m16[:, 0:8], -1.0, lf["lane"], Op.add, Op.is_equal)
+    t_r = run("V", [], v.memset, T.zr[:, :], 1.0)
+    t2 = ts([], lf["yy"], lf["y"], 1.0, lf["y"], Op.add, Op.mult)
+    t = ts([g_m8, g_bm, t_oh], T.t1[:, :], T.m8[:, :], lf["sg"], lf["u"], Op.mult, Op.subtract)
+    ts([], T.oh[:, 8:16], T.m8[:, 0:8], lf["y"], None, Op.is_equal)
+    t_wb = tt([s_wx], T.wb[:, :], T.wx[:, :], T.bm[:, :], Op.mult)
+    t_zr = run("V", [t_r], v.memset, T.zr[:, 0::8], 0.0)
+    ts([t2], lf["mb"], lf["yy"], -2.0, 2.0, Op.mult, Op.add)
+    t_yk = tt([t], T.yk[:, :], T.t1[:, :], T.bm[:, :], Op.mult)
     for j in range(4):
         g_wj = pick([t_wb], mat(T.wj, j), T.wb[:, :], [[0, 8], [1, 4], [0, 4]], Op.is_equal, 0.0, -j, 0)
-    ts([], lf["ym4"], lf["y"], -1.0, -4.0, Op.mult, Op.add)
-    ts([], lf["u1"], lf["u"], -1.0, 1.0, Op.mult, Op.add)
-    ts([], lf["bu"], lf["u"], -BIG, None, Op.mult)
-    ts([], lf["bu1"], lf["u"], BIG, -BIG, Op.mult, Op.add)
-    ts([], lf["tc"], lf["i"], 128.0, -528.0, Op.mult, Op.add)
-    ts([], lf["d0"], lf["i"], 3.0, 512.0, Op.is_equal, Op.mult)
-    ts([], lf["top"], lf["lane"], 15.0, -512.0, Op.is_equal, Op.mult)
-    t_oh = ts([g_m16], T.oh[:, :], T.m16[:, 0:8], -1.0, lf["lane"], Op.add, Op.is_equal)
-    t = ts([t_oh], lf["d"], lf["d0"], lf["top"], -128.0, Op.add, Op.add)
-    t_d8 = ts([t], lf["d8"], lf["d"], 8.0, None, Op.mult)
-    s_g1 = act([g_gm], T.g1[:, 0:127], T.gm[:, 1:128], Fn.Copy, scale=-1.0)
-    t = run("V", [s_g1], v.memset, T.g1[:, 15::16], 0.0)
-    t_nm = tt([t], T.nm[:, :], T.gm[:, :], T.g1[:, :], Op.add)
-    for q in range(8):
-        s_xq = act([t_oh, g_bm], mat(T.xq, q), T.bm[:, :], Fn.Copy, scale=T.oh[:, q:q + 1])
-    s_neg = act([g_id], T.neg[:, :], T.idm[:, :], Fn.Copy, scale=-1.0)
+    g_id = pick([], T.idm[:, :], one, [[-1, 128]], Op.is_equal, 0.0, 0, 1)
+    g_swp = pick([], T.swp[:, :], one, [[-16, 8], [8, 2], [-1, 8]], Op.is_equal, 0.0, -8, 1)
+    own = SW * rank
+    for a, e in [(own + PARTS[1][3] - 8, own + PARTS[1][3]), (own + SW - 8, own + SW)]:
+        t_pad = run("V", [], v.memset, T.ship[:, a:e], 0.0)
+    fix = {n: T.fix[:, a:a + k] for n, a, k in [(-4.0, 0, 512), (4.0, 512, 64), (-16.0, 576, 64), (-32.0, 640, 64)]}
+    for n in fix:
+        s_fix = act([t_one], fix[n], T.ones[:, 0:fix[n].shape[1]], Fn.Copy, scale=n)
+    t = act([g_gm], T.g1[:, 0:127], T.gm[:, 1:128], Fn.Copy, scale=-1.0)
+    s_g1 = act([t], T.g1[:, 15::16], T.ones[:, 0:8], Fn.Copy, scale=0.0)
 
-    for k in range(8):
-        j, y = k // 2, k % 2
-        t = run("V", [ld[k]], v.tensor_copy, T.half[:, :, 32 * j + 16 * y:32 * j + 16 * y + 16], T.raw[:, 8 * k:8 * k + 8, :])
-    s_pw = []
-    for i in range(8):
-        t_let = run("V", [t], v.transpose, T.let[:, i::8], T.half[:, i, :])
-        s_pw.append(act([t_let], mat(T.pw, i), T.let[:, i::8], Fn.Exp, scale=math.log(32.0)))
+    def convert(k):
+        h, at = k // 4, 16 * (k % 4)
+        return run("V", [ld[k]], v.tensor_copy, T.half[:, 8 * h:8 * h + 8, at:at + 16], T.raw[:, 8 * k:8 * k + 8, :])
+
+    def turn(h, deps):
+        t_let.append(run("V", deps, v.transpose, T.let[:, 8 * h:8 * h + 8, :], T.half[:, 8 * h:8 * h + 8, :]))
+        s_pw.append(act([t_let[h]], T.pw[:, 512 * h:512 * h + 512], T.let[:, 8 * h:8 * h + 8, :], Fn.Exp, scale=math.log(32.0)))
+
+    def clamp(h, j):
+        f = T.feat[:, B * j + 512 * h:B * j + 512 * h + 512]
+        t = ts([s_pw[h]], f, T.pw[:, 512 * h:512 * h + 512], 32.0 ** (4 * j - 1), 32.0 ** (4 * j + 3), Op.max, Op.min)
+        return mm([t, g_wj], bank(h), mat(T.wj, j), f, j == 0, j == 3)
+
+    def whole(h, deps):
+        return ts(deps, T.hq[:, 512 * h:512 * h + 512], bank(h), -4.0, None, Op.add)
+
+    def digits(h, deps):
+        cols = slice(512 * h, 512 * h + 512)
+        t_nn.append(tt(deps, T.nn[:, cols], bank(h), T.hq[:, cols], Op.subtract))
+        out = bank(2)[:, 64 * h:64 * h + 64]
+        mm([s_nm, s_fix], out, T.nm[:, :], fix[-32.0], True, False)
+        for i in range(8):
+            t = mm([t_nn[h]], out, T.nm[:, :], nn(h, i), False, i == 7)
+        return t
+
+    def rises(h):
+        e = bank(4 + h)
+        for i in range(8):
+            mm([], e[:, i::8], T.gm[:, :], nn(h, i), False, False)
+            if i:
+                mm([], e[:, i::8], T.g1[:, :], nn(h, i - 1), False, False)
+
+    def offsets(h):
+        e = bank(4 + h)
+        mm([s_nm, s_fix], e, T.nm[:, :], fix[-4.0], True, False)
+        mm([], e[:, 0::8], T.idm[:, :], fix[-16.0], False, False)
+        mm([], e[:, 0::8], T.g1[:, :], fix[4.0], False, False)
+
+    def nn(h, i):
+        return T.nn[:, 512 * h + 64 * i:512 * h + 64 * i + 64]
+
+    def keys_of(h):
+        for i in range(8):
+            t = act([t_oh], own_keys[:, 512 * h + i:512 * h + 512:8], T.let[:, 8 * h + i, :], Fn.Identity, bias=lf["x16"])
+        leave([t], "k%d" % h)
+        return t
+
+    t_let, s_pw, t_nn = [], [], []
     own_keys = T.keyw[:, B * rank:B * rank + B]
-    t_key = ts([t_let, t_x16], own_keys, T.let[:, :], lf["x16"], None, Op.add)
-    t_dup = [dma("Y", [t_key], "dup", T.keyw[:, STR + B * rank:STR + B * rank + B], own_keys)]
-    send([t_key], own_keys[:, 0:KD], own_keys[:, 0:KD], "kin%d" % rank)
-    leave([], 0, "hk")
-    act([t_d8], T.no[:, :], T.onef[:, :], Fn.Copy, scale=lf["d8"])
-    t = act([], T.ck[:, :], T.ones[:, 0:512], Fn.Copy, scale=lf["d"])
-    t_ck = act([t], T.ck[:, 0::8], T.ones[:, 0:64], Fn.Copy, scale=lf["tc"])
-    act([], T.b16[:, :], T.bm[:, :], Fn.Copy, scale=0.0625)
-    s_b32 = act([], T.b32[:, :], T.bm[:, :], Fn.Copy, scale=0.03125)
-    t_zt = [act([], T.zt[:, ZW * k:ZW * k + ZW], T.ones[:, :], Fn.Copy, scale=lf["bu" if k % 2 else "bu1"]) for k in range(6)]
+    turn(0, [convert(k) for k in range(4)])
+    keys_of(0)
+    convert(4)
+    convert(5)
+    mm([s_g1, g_id], bank(3)[:, 0:128], T.idm[:, :], T.gm[:, :], True, False)
+    t = mm([], bank(3)[:, 0:128], T.idm[:, :], T.g1[:, :], False, True)
+    s_nm = act([t], T.nm[:, :], bank(3)[:, 0:128], Fn.Copy)
+    clamp(0, 0)
+    offsets(0)
+    turn(1, [convert(k) for k in range(6, 8)])
+    t_key = keys_of(1)
     for u in range(2):
         g_wu = pick([], mat(T.wu, u), one, [[-16, 8], [0, 2], [-1, 8]], Op.is_equal, 0.0, -8 * u, 1)
     t = pick([], T.t3[:, :], T.onef[:, :], [[-16, 8], [0, 16]], Op.is_ge, 0.0, 0, 1)
-    pick([t], T.lt[:, :], T.t3[:, :], [[1, 128]], Op.is_gt, 0.0, 0, -1)
+    g_lt = pick([t], T.lt[:, :], T.t3[:, :], [[1, 128]], Op.is_gt, 0.0, 0, -1)
+    t_d0 = [clamp(0, j) for j in range(1, 4)]
+    for q in range(8):
+        s_xq = act([g_bm], mat(T.xq, q), T.bm[:, :], Fn.Copy, scale=T.oh[:, q:q + 1])
+    for q in range(8):
+        act([t_yk], mat(T.mq, q), T.yk[:, :], Fn.Copy, scale=T.oh[:, 8 + q:9 + q])
+    act([], T.n4[:, :], T.idm[:, :], Fn.Copy, scale=-4.0)
+    t_zt = [act([], T.zt[:, ZW * k:ZW * k + ZW], T.ones[:, :], Fn.Copy, scale=lf["bu" if k % 2 else "bu1"]) for k in range(2)]
+    s_nsw = act([g_swp], T.nsw[:, :], T.swp[:, :], Fn.Copy, scale=-1.0)
+    act([], T.b16[:, :], T.bm[:, :], Fn.Copy, scale=0.0625)
+    s_b32 = act([], T.b32[:, :], T.bm[:, :], Fn.Copy, scale=0.03125)
+    clamp(1, 0)
+    clamp(1, 1)
+    offsets(1)
+    run("V", [lpat], v.tensor_copy, T.cl[:, 0:128], T.pat[:, 0:128])
+    t_h0 = whole(0, t_d0)
+    clamp(1, 2)
+    t_d1 = clamp(1, 3)
+    digits(0, [t_h0])
+    t_cl = run("V", [], v.tensor_copy, T.cl[:, 128:256], T.pat[:, 128:256])
+    rises(0)
+    t_h1 = whole(1, [t_d1])
+    t = ts([lst], T.s1[:, :], T.sti[:, :], 15, None, Op.bitwise_and)
+    t_sb = digits(1, [t_h1])
+    ts([], T.s2[:, :], T.sti[:, :], 4, None, Op.arith_shift_right)
+    t_s3 = ts([], T.s3[:, :], T.pat[:, 0:32], 8.0, float(STR), Op.is_ge, Op.mult)
+    t_kc = ts([t], T.kc[:, :], T.s1[:, :], 0.0625, None, Op.mult)
+    t_vr = run("V", [t_sb], v.tensor_tensor_scan, T.vr[:, 1:129], one, bank(2)[:, 0:128], 0.0, Op.mult, Op.add)
+    t_tot = run("V", [t_vr], v.tensor_copy, T.tot[:, 4 * rank:4 * rank + 4], T.vr[:, 128:132])
+    leave([t_tot], "tv")
     g_le = pick([], T.le[:, :], T.t3[:, :], [[1, 128]], Op.is_ge, 0.0, 0, -1)
-    g_swp = pick([], T.swp[:, :], one, [[-16, 8], [8, 2], [-1, 8]], Op.is_equal, 0.0, -8, 1)
-
-    t_d = []
-    for h in range(2):
-        for j in range(4):
-            f = T.feat[:, B * j + 512 * h:B * j + 512 * h + 512]
-            t = ts([s_pw[4 * h + 3]], f, T.pw[:, 512 * h:512 * h + 512], 32.0 ** (4 * j - 1), 32.0 ** (4 * j + 3), Op.max, Op.min)
-            t = mm([t, g_wj], bank(h), mat(T.wj, j), f, j == 0, j == 3)
-        t_d.append(t)
-    t_nn = []
-    for h in range(2):
-        cols = slice(512 * h, 512 * h + 512)
-        t = ts([t_d[h]], T.hq[:, cols], bank(h), -4.0, None, Op.add)
-        t_nn.append(tt([t], T.nn[:, cols], bank(h), T.hq[:, cols], Op.subtract))
-        for i in range(4 * h, 4 * h + 4):
-            t_sb = mm([t_nn[h], t_nm], bank(2)[:, 0:128], T.nm[:, :], mat(T.nn, i), i == 0, i == 7)
-        if h == 0:
-            run("V", [], v.memset, T.vr[:, 0:1], 0.0)
-            run("V", [], v.memset, T.vr[:, 129:132], 0.0)
-    t_cl = run("V", [lpat], v.tensor_copy, T.cl[:, :], T.pat[:, :])
-    t_vr = run("V", [t_sb, t_ck], v.tensor_tensor_scan, T.vr[:, 1:129], T.no[:, :], bank(2)[:, 0:128], 0.0, Op.add, Op.add)
-    mine = T.tot[:, 4 * rank:4 * rank + 4]
-    send([t_vr], T.vr[:, 128:132], mine, "tin")
-    t_tot = run("V", [t_vr], v.tensor_copy, mine, T.vr[:, 128:132])
+    for buf, a, e, n in [(T.keyw, NB, STR, 1024), (T.keyw, STR + NB, W, 1024), (T.base, NB + 1, STR, 0), (T.base, STR + NB + 1, W, 0)]:
+        t_fill = run("G", [], g.iota, buf[:, a:e], [[0, e - a]], n, 0, **fl)
 
     for u in range(2):
         t = mm([t_cl, g_wu], bank(7)[:, u::2], mat(T.wu, u), T.cl[:, :], True, True)
     s_cd = act([t], T.cd[:, :], bank(7), Fn.Copy)
-    s_nsw = act([g_swp], T.nsw[:, :], T.swp[:, :], Fn.Copy, scale=-1.0)
-    s_ab = []
-
-    def letters(st):
-        for q in range(8):
-            t = mm([s_cd, s_xq, t_nn[1]] + s_ab[st - 2:st - 1], bank(st % 2)[:, q::8], mat(T.xq, q), T.cd[:, 64 * st:64 * st + 64], True, True)
-        s_ab.append(act([t], T.ab[:, 512 * st:512 * st + 512], bank(st % 2), Fn.Abs, bias=lf["ym4"]))
-
-    for h in range(2):
-        e = bank(4 + h)
-        mm([t_ck, g_id], e, T.idm[:, :], T.ck[:, :], True, False)
-        for i in range(8):
-            mm([t_nn[1]], e[:, i::8], T.gm[:, :], mat(T.nn, i)[:, 64 * h:64 * h + 64], False, False)
-            if i:
-                mm([], e[:, i::8], T.g1[:, :], mat(T.nn, i - 1)[:, 64 * h:64 * h + 64], False, False)
-    for st in range(EARLY):
-        letters(st)
-    own = SW * rank
-    t = run("V", [], v.memset, T.zr[:, :], 1.0)
-    run("V", [], v.memset, T.ship[:, own + PARTS[1][2]:own + PARTS[1][3]], 0.0)
-    t_pad = run("V", [], v.memset, T.ship[:, own + SW - 8:own + SW], 0.0)
-    t_zr = run("V", [t], v.memset, T.zr[:, 0::8], 0.0)
-    t_z = run("V", [], v.memset, T.zs[:, :], -4 * SEL)
-    ts([], lf["sl"], lf["u"], SEL, -SEL, Op.mult, Op.add)
-    ts([], lf["zs"], lf["u"], -5 * SEL, SEL, Op.mult, Op.add)
-    for x in range(2):
-        mine = [p for p in SHARE[x] if p[0] == "V"]
-        a, k = mine[0][1:] if mine else (1, 1)
-        t = ts([], T.li[:, 4 + x:5 + x], T.lp[:, :], k - 1, None, Op.bitwise_and)
-        t_k = ts([t], T.kap[:, x:x + 1], T.li[:, 4 + x:5 + x], float(a), 0.5, Op.not_equal, Op.mult)
-    ts([lst], T.s1[:, :], T.sti[:, :], 15, None, Op.bitwise_and)
-    ts([t_k], T.kap[:, 2:4], T.kap[:, 0:2], -1.0, 0.46875, Op.mult, Op.add)
-    ts([], T.kap[:, 4:6], T.kap[:, 0:2], -1.0, None, Op.mult)
-    t = ts([], T.kap[:, 6:8], T.kap[:, 0:2], lf["sl"], None, Op.add)
-    t_zs = ts([t_z], T.zs[:, 1::2], T.onef[:, 0:32], lf["zs"], None, Op.mult)
-    t_kap = ts([t], T.kap[:, 8:10], T.kap[:, 6:8], -0.46875, None, Op.add)
-    kap = {n: [T.kap[:, 2 * k + x:2 * k + x + 1] for x in range(2)] for k, n in enumerate(["k", "c", "n", "y", "o"])}
-    ts([], T.s2[:, :], T.sti[:, :], 4, None, Op.arith_shift_right)
-    t = ts([], T.s3[:, :], T.pat[:, 0:32], 8.0, float(STR), Op.is_ge, Op.mult)
-    t_kc = ts([], T.kc[:, :], T.s1[:, :], 0.0625, None, Op.mult)
-    for x in range(2):
-        t2 = tt([t], T.s4[:, 32 * x:32 * x + 32], T.s2[:, 32 * x:32 * x + 32], T.s3[:, :], Op.add)
-    run("V", [], v.memset, T.keyw[:, NB:STR], 1024.0)
-    run("V", [], v.memset, T.keyw[:, STR + NB:W], 1024.0)
-    t = run("V", [t2], v.tensor_copy, T.off[:, 0:64], T.s4[:, :])
-    run("V", [], v.memset, T.base[:, NB + 1:STR], 0.0)
-    t_fill = run("V", [], v.memset, T.base[:, STR + NB + 1:W], 0.0)
-    t_ch = ts([s_cd], T.ch[:, :], T.cd[:, :], 8.0, float(STR), Op.is_ge, Op.mult)
-    t_of, t_kl, t_m = [t, t], [], []
+    t_ch = act([], T.ch[:, :], bank(7), Fn.Sign, bias=-7.5)
+    rises(1)
+    mm([s_cd], bank(6), T.idm[:, :], T.cd[:, :], True, False)
+    t = mm([t_ch], bank(6), T.n4[:, :], T.ch[:, :], False, True)
+    act([], T.ih[:, :], T.idm[:, :], Fn.Copy, scale=STR / 2)
+    s_neg = act([], T.neg[:, :], T.idm[:, :], Fn.Copy, scale=-1.0)
+    t_zt += [ts([], T.zt[:, ZW * k:ZW * k + ZW], T.ones[:, :], lf["bu" if k % 2 else "bu1"], None, Op.mult) for k in range(2, 4)]
+    s_sq = act([t], T.sq[:, :], bank(6), Fn.Square, bias=lf["sb"])
+    t_m = []
 
     def masks(st):
-        t_m.append(ts([s_ab[st]], T.msk[:, 512 * st:512 * st + 512], T.ab[:, 512 * st:512 * st + 512], 4.0, 2.0, Op.is_equal, Op.mult))
+        for q in range(8):
+            t = mm([s_sq, t_nn[1]] + t_m[st - 2:st - 1], bank(st % 2)[:, q::8], mat(T.mq, q), T.sq[:, 64 * st:64 * st + 64], True, True)
+        t_m.append(act([t], T.msk[:, 512 * st:512 * st + 512], bank(st % 2), Fn.Relu, scale=2.0, bias=lf["mb"]))
 
-    for st in range(MASKS):
+    t_z = run("V", [], v.memset, T.zs[:, :], -4 * SEL)
+    ts([], lf["kc"], lf["odd"], -0.5, 0.46875, Op.mult, Op.add)
+    ts([], lf["kn"], lf["odd"], -0.5, None, Op.mult)
+    t = ts([], lf["ky"], lf["odd"], 0.5, lf["sl"], Op.mult, Op.add)
+    t_zs = ts([t_z], T.zs[:, 1::2], T.onef[:, 0:32], lf["zs"], None, Op.mult)
+    t_kap = ts([t], lf["ko"], lf["ky"], STR / 2 - 0.46875, None, Op.add)
+    kap = {n: [lf["k" + n]] * 2 for n in "cnyo"}
+    for x in range(2):
+        t2 = tt([t_s3], T.s4[:, 32 * x:32 * x + 32], T.s2[:, 32 * x:32 * x + 32], T.s3[:, :], Op.add)
+    t = run("V", [t2], v.tensor_copy, T.off[:, 0:64], T.s4[:, :])
+    t_of, t_kl = [t, t], []
+    t_dup = [run("V", [t_key], v.tensor_copy, T.keyw[:, STR + B * rank:STR + B * rank + B], own_keys)]
+    for st in range(EARLY):
         masks(st)
 
     cols = T.tot[:, 0:4 * R:4]
@@ -378,30 +417,32 @@ def rank_program(g, core, T, topo):
         mm([("tin", width * (R - 1)), t_tot, g_le], bank(3)[:, 0:rank], T.le[:, :], cols[:, 0:rank], True, True)
     t = mm([("tin", width * (R - 1)), t_tot, g_le], bank(3)[:, rank:R], T.lt[:, :], cols[:, rank:R], True, True)
     t = run("V", [t], v.tensor_reduce, T.init[:, :], bank(3)[:, 0:R], AxisListType.X, Op.add)
+    masks(EARLY)
     val = bank(2)[:, 256:385]
-    t_hb = ts([t], T.hb[:, 1:130], T.vr[:, 0:129], T.init[:, :], 256.0, Op.add, Op.max)
+    t_hb = ts([t], T.hb[:, 0:129], T.vr[:, 0:129], T.init[:, :], 256.0, Op.add, Op.max)
     t = ts([], val, T.vr[:, 0:129], T.init[:, :], None, Op.add)
-    t_rb = tt([t], T.rb[:, 0:129], val, T.hb[:, 1:130], Op.subtract)
-    t_e2 = [mm([t_rb], bank(4 + h)[:, 0::8], T.idm[:, :], T.rb[:, 64 * h:64 * h + 64], False, True) for h in range(2)]
+    t_rb = tt([t], T.rb[:, 0:129], val, T.hb[:, 0:129], Op.subtract)
     s_dh = []
     for b0, n, at, low, end in PARTS:
         a, k = b0 // 8, (n + 7) // 8
         out = bank(6)[:, a:a + k]
-        mm([t_hb, s_nsw], out, T.swp[:, :], T.hb[:, 1 + a:1 + a + k], True, False)
-        t = mm([], out[:, 1:], T.nsw[:, :], T.hb[:, 1 + a:a + k], False, True)
+        mm([t_hb, s_nsw, s_sq], out, T.swp[:, :], T.hb[:, a:a + k], True, False)
+        t = mm([], out[:, 1:], T.nsw[:, :], T.hb[:, a:a + k - 1], False, True)
+    t_e2 = [mm([t_rb], bank(4 + h)[:, 0::8], T.idm[:, :], T.rb[:, 64 * h:64 * h + 64], False, True) for h in range(2)]
     for b0, n, at, low, end in PARTS:
         a, k = b0 // 8, (n + 7) // 8
         s_dh.append(act([t, t_pad], T.ship[:, own + at:own + at + k], bank(6)[:, a:a + k], Fn.Copy))
     lo_a, lo_b = own + PARTS[0][3], own + PARTS[1][3]
     scan = v.tensor_tensor_scan
-    t_la = run("V", [t_e2[0], t_zr], scan, T.ship[:, lo_a:lo_a + HC], T.zr[:, 0:HC], bank(4)[:, 0:HC], 0.0, Op.mult, Op.add)
-    leave([t_la, s_dh[0]], 1, "hl")
-    if HC < 512:
-        run("V", [], scan, T.ship[:, lo_b:lo_b + 512 - HC], T.zr[:, 0:512 - HC], bank(4)[:, HC:512], 0.0, Op.mult, Op.add)
-    run("V", [t_pad], v.tensor_copy, T.ship[:, lo_b + B - HC:lo_b + B - HC + 1], T.rb[:, 128:129])
-    t_lb = run("V", [t_e2[1]], scan, T.ship[:, lo_b + 512 - HC:lo_b + B - HC], T.zr[:, :], bank(5), 0.0, Op.mult, Op.add)
-    part_b = T.ship[:, own + PARTS[1][2]:own + SW]
-    send([t_lb, s_dh[1]], part_b, part_b, "lb%d" % rank)
+    run("V", [t_pad, t_rb], v.tensor_copy, T.ship[:, lo_b + B - HC:lo_b + B - HC + 1], T.rb[:, 128:129])
+    cuts = sorted({0, 512, HC, B})
+    for a, e in zip(cuts, cuts[1:]):
+        to = lo_a + a if a < HC else lo_b + a - HC
+        t_lb = run("V", [t_e2[a // 512], t_zr], scan, T.ship[:, to:to + e - a], T.zr[:, 0:e - a], T.pb[:, a:e], 0.0, Op.mult, Op.add)
+        if e == HC:
+            t_la = t_lb
+            leave([t_la, s_dh[0]], "la")
+    leave([t_lb, s_dh[1]], "lb")
 
     used = {}
 
@@ -413,20 +454,20 @@ def rank_program(g, core, T, topo):
             z = T.zt[:, ZW * (2 * slot + chi):ZW * (2 * slot + chi) + n]
             t = act(deps + [t_zt[2 * slot + chi]] + used.get((slot, chi), []), z[:, 0::8], T.ship[:, SW * r + at:SW * r + at + k], Fn.Identity,
                     scale=lf["u1" if chi else "u"], bias=lf["bu" if chi else "bu1"])
-            to = STR * chi + B * r + b0
-            t = run("V", deps + [t], scan, T.base[:, to:to + n], z, T.ship[:, SW * r + low:SW * r + low + n], 0.0, Op.add, Op.max)
+            to = T.base[:, STR * chi + B * r + b0:STR * chi + B * r + b0 + n]
+            t = run("V", deps + [t], scan, to, z, T.ship[:, SW * r + low:SW * r + low + n], 0.0, Op.add, Op.max)
             used[slot, chi] = [t]
         return t
 
+    unfold(rank, 0, 0, [t_la, s_dh[0]])
+    unfold(rank, 1, 1, [t_lb, s_dh[1]])
     for q in range(8):
         t_e = pick([s_b32], mat(T.e32, q), T.b32[:, :], [[0, 16], [1, 8]], Op.is_equal, 0.0, -q, 0)
     for q in range(8):
         if any(e == "V" and q % k == a for x in range(2) for e, a, k in SHARE[x]):
             t_e = pick([], mat(T.e16, q), T.b16[:, :], [[0, 16], [1, 8]], Op.is_equal, 0.0, -q, 0)
-    unfold(rank, 0, 0, [t_la, s_dh[0]])
-    unfold(rank, 1, 1, [t_lb, s_dh[1]])
-    for st in range(EARLY, 8):
-        letters(st)
+    for st in range(EARLY + 1, 8):
+        masks(st)
     for x in range(2):
         for u in range(2):
             out = bank(7)[:, 64 * x + u:64 * x + 64:2]
@@ -434,25 +475,13 @@ def rank_program(g, core, T, topo):
             t = mm([], out, mat(T.wu, u), T.cl[:, 0:32], False, True)
     for x in range(2):
         t_kl.append(act([t, t_kap], T.kl[:, 64 * x:64 * x + 64], bank(7)[:, 64 * x:64 * x + 64], Fn.Identity, bias=kap["n"][x]))
-    for st in range(MASKS, 8):
-        masks(st)
-    ring = [(rank + k) % R for k in range(1, R)]
-    for r, q in zip(ring, DUP):
-        deps = [("kin%d" % r, width + hw)]
-        to, src = T.keyw[:, STR + B * r:STR + B * r + B], T.keyw[:, B * r:B * r + B]
-        if q == "V":
-            t_dup.append(run("V", deps, v.tensor_copy, to, src))
-        elif q == "S":
-            t_dup.append(act(deps, to, src, Fn.Copy))
-        else:
-            t_dup.append(dma("Y", deps, "dup", to, src))
-    t_dup = [t if t[0] != "dup" else ("dup", total["dup"]) for t in t_dup]
-    for part, sem, n in [(1, "lb", width), (0, "la", hw)]:
-        for slot, r in enumerate(ring):
-            t_base = unfold(r, part, slot, [("%s%d" % (sem, r), n)])
-        if part:
-            for x in range(2):
-                s_clb = act([t_kap, s_cd], T.clb[:, 512 * x + 64:512 * x + 512], T.cd[:, 64:512], Fn.Identity, bias=kap["c"][x])
+    s_clb = run("V", [t_kap, s_cd], v.tensor_scalar, T.clb[:, 64:512], T.cd[:, 64:512], kap["c"][0], None, Op.add)
+    for k in range(1, R):
+        r = (rank - k) % R
+        t_dup = [run("V", [landed("kin%d" % r)], v.tensor_copy, T.keyw[:, STR + B * r:STR + B * r + B], T.keyw[:, B * r:B * r + B])]
+    for n, (part, k) in enumerate([(1, 1), (1, 2), (0, 1), (0, 2), (1, 3), (0, 3)]):
+        r = (rank - k) % R
+        t_base = [unfold(r, part, n % 2, [landed("%s%d" % ("lb" if part else "la", r))])]
 
     P = [bank(6)[:, 0:64], bank(7)[:, 0:64]]
     banks = [{"V": bank(0), "S": bank(1)}, {"V": bank(2), "S": bank(3)}]
@@ -479,7 +508,7 @@ def rank_program(g, core, T, topo):
         tk[x]["kg"] = act([t_of[x], t_fill] + t_dup, kg[x], T.keyw[:, 0:W].indirect(offs(x, st)), Fn.Copy)
 
     def bases(x, st, a, e):
-        tk[x]["ym"] = tt([t_of[x], t_m[st], t_base], ym[x][:, 16 * a:16 * e], T.base[:, 0:W].indirect(offs(x, st)[:, a:e]),
+        tk[x]["ym"] = tt([t_of[x], t_m[st], t_fill] + t_base, ym[x][:, 16 * a:16 * e], T.base[:, 0:W].indirect(offs(x, st)[:, a:e]),
                          T.msk[:, 512 * st + 16 * a:512 * st + 16 * e], Op.mult)
 
     def spread(x, st, deps=()):
@@ -490,7 +519,7 @@ def rank_program(g, core, T, topo):
             tk[x]["sp"] = mm([t_kl[x]] + list(deps), banks[x][e][:, c], mat(T.xq, q), T.kl[:, 64 * x:64 * x + 64], alone or e not in begun, alone)
             begun.add(e)
         if st < 7:
-            mm([t_ch], P[x], T.idm[:, :], T.ch[:, 64 * st + 64:64 * st + 128], True, False)
+            mm([t_ch], P[x], T.ih[:, :], T.ch[:, 64 * st + 64:64 * st + 128], True, False)
 
     def minus(x):
         mine = [p for p in lay[x][1] if p[0] == "S"]
@@ -498,8 +527,8 @@ def rank_program(g, core, T, topo):
             tk[x]["ng"] = mm([tk[x]["kg"], s_neg], banks[x]["S"][:, at:at + n], T.neg[:, :], kg[x][:, a::k], False, at == mine[-1][3])
 
     def compare(x, e):
-        if e == "S":
-            n = lay[x][2]["S"]
+        n = lay[x][2]["S"]
+        if e == "S" and n:
             tk[x]["S"] = act([tk[x]["ng"]], xs[x]["S"][:, 0:n], banks[x]["S"][:, 0:n], Fn.Sign, bias=0.46875)
         for e2, a, k, at, n in lay[x][1]:
             if e == e2 == "V":
@@ -512,13 +541,14 @@ def rank_program(g, core, T, topo):
     def sum_signs(x, e):
         qs = [q for q in range(8) if lay[x][0][q][0] == e]
         for q in qs:
-            tk[x]["P"] = mm([tk[x][e]], P[x], mat(T.e32 if e == "S" else T.e16, q), xs[x][e][:, lay[x][0][q][1]], False, e == "S" and q == qs[-1])
+            tk[x]["P"] = mm([tk[x][e]], P[x], mat(T.e32 if e == "S" else T.e16, q), xs[x][e][:, lay[x][0][q][1]], False,
+                            q == qs[-1] and (e == "S" or len(qs) == 8))
 
     def choose(x, st):
         sel, oi = T.sel[:, 64 * x:64 * x + 64], T.oi[:, 64 * x:64 * x + 64]
         t = run("V", [tk[x]["P"], t_zs], scan, sel, T.zs[:, :], P[x], 0.0, Op.add, Op.max)
         if st < 7:
-            t2 = tt([s_clb], oi, P[x], T.clb[:, 512 * x + 64 * st + 64:512 * x + 64 * st + 128], Op.subtract)
+            t2 = tt([s_clb], oi, P[x], T.clb[:, 64 * st + 64:64 * st + 128], Op.subtract)
             t_of[x] = ts([t], offs(x, st + 1), sel[:, 1::2], kap["o"][x], None, Op.add)
             t_kl[x] = tt([t2], T.kl[:, 64 * x:64 * x + 64], P[x], oi, Op.subtract)
         else:
@@ -531,11 +561,11 @@ def rank_program(g, core, T, topo):
         if st:
             sum_signs(Z, "S")
             choose(Z, st - 1)
-        spread(A, st, [] if st else [s_ab[7], t_kl[1], t_lb])
-        minus(A)
+        spread(A, st, [] if st else [t_m[7], t_kl[1], t_lb, s_neg])
         keys(Z, st)
         bases(A, st, 16, 32)
         spread(Z, st)
+        minus(A)
         compare(A, "V")
         sum_bases(A, st)
         sum_signs(A, "V")
@@ -552,5 +582,5 @@ def rank_program(g, core, T, topo):
     choose(Z, 7)
     dma("Y", t_of, "out", T.y[:, :], T.yo[:, :])
 
-    for sem in ["cV", "cS", "cP", "cG", "out", "snt", "dup"]:
+    for sem in ["cV", "cS", "cP", "cG", "out", "snt"]:
         need("G", [(sem, total[sem])])

import math
from concourse.bass import DstId, RemoteDMATransfer
from concourse.mybir import AluOpType as Op, ActivationFunctionType as Fn, AxisListType

R, B = 4, 1024
NB = R * B
STR = 4224
W = 2 * STR
HC = 448
EARLY = 1
BIG = 131072.0
SEL = 16384.0
PARTS = [(0, HC, 0, HC // 8, HC // 8 + HC),
         (HC, B + 1 - HC, HC // 8 + HC, HC // 8 + HC + (B - HC) // 8 + 8, HC // 8 + HC + (B - HC) // 8 + B - HC + 16)]
SW = PARTS[1][4]
ZW = max(HC, B - HC) + 8
SHARE = [[("V", 0, 2), ("S", 1, 2)], [("V", 0, 2), ("S", 1, 2)]]

bf, f32, i32 = "bfloat16", "float32", "int32"
SCRATCH = {
    "raw": ("sbuf", [128, 64, 16], i32),
    "half": ("sbuf", [128, 16, 64], bf),
    "let": ("sbuf", [128, 16, 64], bf),
    "pw": ("sbuf", [128, B], bf),
    "feat": ("sbuf", [128, 4 * B], bf),
    "hq": ("sbuf", [128, B], i32),
    "nn": ("sbuf", [128, B], bf),
    "keyw": ("sbuf", [128, W], bf),
    "base": ("sbuf", [128, W], bf),
    "ship": ("sbuf", [128, R * SW], bf),
    "zt": ("sbuf", [128, 4 * ZW], bf),
    "vr": ("sbuf", [128, 132], f32),
    "tot": ("sbuf", [128, 4 * R], f32),
    "init": ("sbuf", [128, 1], f32),
    "le": ("sbuf", [128, 128], f32),
    "hb": ("sbuf", [128, 130], bf),
    "rb": ("sbuf", [128, 130], bf),
    "ones": ("sbuf", [128, ZW], bf),
    "onef": ("sbuf", [128, 128], f32),
    "c32": ("sbuf", [128, 128], bf),
    "lp": ("sbuf", [128, 1], i32),
    "li": ("sbuf", [128, 8], i32),
    "lf": ("sbuf", [128, 24], f32),
    "m16": ("sbuf", [128, 128], bf),
    "wx": ("sbuf", [128, 128], bf),
    "wb": ("sbuf", [128, 128], bf),
    "wj": ("sbuf", [128, 4 * 128], bf),
    "t1": ("sbuf", [128, 128], bf),
    "t2": ("sbuf", [128, 128], bf),
    "t3": ("sbuf", [128, 128], f32),
    "bm": ("sbuf", [128, 128], bf),
    "b32": ("sbuf", [128, 128], bf),
    "b16": ("sbuf", [128, 128], bf),
    "kap": ("sbuf", [128, 10], f32),
    "oh": ("sbuf", [128, 16], f32),
    "m8": ("sbuf", [128, 128], bf),
    "yk": ("sbuf", [128, 128], bf),
    "n4": ("sbuf", [128, 128], bf),
    "ih": ("sbuf", [128, 128], bf),
    "mq": ("sbuf", [128, 8 * 128], bf),
    "gm": ("sbuf", [128, 128], bf),
    "g1": ("sbuf", [128, 128], bf),
    "nm": ("sbuf", [128, 128], bf),
    "lt": ("sbuf", [128, 128], f32),
    "idm": ("sbuf", [128, 128], bf),
    "neg": ("sbuf", [128, 128], bf),
    "swp": ("sbuf", [128, 128], bf),
    "nsw": ("sbuf", [128, 128], bf),
    "wu": ("sbuf", [128, 2 * 128], bf),
    "xq": ("sbuf", [128, 8 * 128], bf),
    "e16": ("sbuf", [128, 8 * 128], bf),
    "e32": ("sbuf", [128, 8 * 128], bf),
    "fix": ("sbuf", [128, 704], bf),
    "zr": ("sbuf", [128, 512], bf),
    "zs": ("sbuf", [128, 64], f32),
    "pat": ("sbuf", [128, 256], i32),
    "cl": ("sbuf", [128, 256], bf),
    "cd": ("sbuf", [128, 512], bf),
    "ch": ("sbuf", [128, 512], bf),
    "sq": ("sbuf", [128, 512], bf),
    "clb": ("sbuf", [128, 512], f32),
    "msk": ("sbuf", [128, 8 * 512], bf),
    "sti": ("sbuf", [128, 64], i32),
    "s1": ("sbuf", [128, 64], i32),
    "s2": ("sbuf", [128, 64], i32),
    "s3": ("sbuf", [128, 32], f32),
    "s4": ("sbuf", [128, 64], f32),
    "kc": ("sbuf", [128, 64], bf),
    "sel": ("sbuf", [128, 128], f32),
    "oi": ("sbuf", [128, 128], i32),
    "kl": ("sbuf", [128, 128], bf),
    "off": ("sbuf", [128, 128], "uint16"),
    "kg": ("sbuf", [128, 1024], bf),
    "ym": ("sbuf", [128, 1024], bf),
    "xs": ("sbuf", [128, 1024], bf),
    "yo": ("sbuf", [128, 64], f32),
    "pa": ("psum", [128, 2048], f32),
    "pb": ("psum", [128, 2048], f32),
}
SEMAPHORES = (["cV", "cS", "cP", "cG", "lpat", "lst", "out", "k0", "k1", "tv", "la", "tin", "snt"] + ["ld%d" % k for k in range(8)]
              + ["%s%d" % (n, r) for n in ("kin", "la", "lb") for r in range(R)])


def helpers(rank_core, T, topo):
    return [c for c in topo.cores_of(rank_core)
            if c != rank_core and all(topo.may_write(c, d) for d in T.cores if d != rank_core)]


def route(core, to, topo):
    ids, mask = [], None
    for c in to:
        rid, pid = topo.addr(c)[:2]
        ids.append(DstId(rid=rid, pnc=pid))
        mask = topo.mask(core, c) if mask is None else mask & topo.mask(core, c)
    return ids, mask, bin(mask).count("1")


def deal(mask, n):
    bits = [e for e in range(mask.bit_length()) if mask >> e & 1]
    k = len(bits) // n
    return [sum(1 << e for e in bits[k * i:k * i + k]) for i in range(n)]


def ways(rank, T, topo):
    home = T.cores[rank]
    hands = helpers(home, T, topo)
    near = [c for c in hands if topo.die(c) == topo.die(home)]
    far = [c for c in hands if c not in near]
    away = route(home, [c for c in T.cores if c != home], topo)[1]
    every = route(home, hands, topo)[1]
    stay = every & ~away

    def cut(buf, at, n, to, masks):
        k = n // len(to)
        return [(buf[:, at + k * i:at + k * i + k], c, m) for i, (c, m) in enumerate(zip(to, masks))]

    return {"k0": ("kin%d" % rank, cut(T.keyw, B * rank, B // 2, far, deal(stay, len(far)))),
            "k1": ("kin%d" % rank, cut(T.keyw, B * rank + B // 2, B // 2, [None] + near, [away] + deal(stay, len(near)))),
            "tv": ("tin", cut(T.tot, 4 * rank, 4, [None], [away])),
            "la": ("la%d" % rank, cut(T.ship, SW * rank, PARTS[0][4], far, deal(every, len(far)))),
            "lb": ("lb%d" % rank, cut(T.ship, SW * rank + PARTS[0][4], SW - PARTS[0][4], [None], [away]))}


def hand_on(g, core, rank, T, topo):
    ids, mask, width = route(core, [T.cores[(rank + k) % R] for k in range(1, R)], topo)
    sent = 0
    for name, (there, parts) in ways(rank, T, topo).items():
        for piece, hand, came in parts:
            if hand == core:
                g.wait_ge(T.sem[name], bin(came).count("1"))
                g.remote_dma_fused([RemoteDMATransfer(dst_ids=ids, dma_engine_mask=mask, remote_sem=T.sem[there],
                                                      srcs=[piece], dsts=[piece for _ in ids], alu_op=0)],
                                   local_sem=T.sem.snt)
                sent += width
    g.wait_ge(T.sem.snt, sent)


def rank_program(g, core, T, topo):
    rank = T.rank_of(core)
    if rank is None:
        for r, c in enumerate(T.cores):
            if core in helpers(c, T, topo):
                hand_on(g, core, r, T, topo)
        return
    queues = {"V": g.vector, "S": g.scalar, "P": g.tensor, "G": g, "Y": g.sync}
    total, seen = {}, {}

    def need(q, deps):
        for sem, val in deps:
            if seen.get((q, sem), 0) < val:
                queues[q].wait_ge(T.sem[sem], val)
                seen[(q, sem)] = val

    def run(q, deps, f, *a, **kw):
        need(q, deps)
        sem = "c" + q
        f(*a, **kw).then_inc(T.sem[sem], 1)
        total[sem] = total.get(sem, 0) + 1
        return (sem, total[sem])

    def dma(q, deps, sem, out, in_):
        need(q, deps)
        queues[q].dma_start(out, in_).then_inc(T.sem[sem], 16)
        total[sem] = total.get(sem, 0) + 16
        return (sem, total[sem])

    v, s, pe = g.vector, g.scalar, g.tensor

    def ts(deps, *a):
        return run("V", deps, v.tensor_scalar, *a)

    def tt(deps, *a):
        return run("V", deps, v.tensor_tensor, *a)

    def act(deps, *a, **kw):
        return run("S", deps, s.activation, *a, **kw)

    def mm(deps, *a):
        return run("P", deps, pe.matmul, *a)

    def pick(deps, *a):
        return run("G", deps, g.affine_select, *a)

    def mat(buf, k):
        return buf[:, 128 * k:128 * k + 128]

    def bank(k):
        return (T.pa if k < 4 else T.pb)[:, 512 * (k % 4):512 * (k % 4) + 512]

    others = [T.cores[(rank + k) % R] for k in range(1, R)]
    ids, mask, width = route(core, others, topo)
    calls = ways(rank, T, topo)

    def landed(sem):
        r = int(sem[-1])
        return (sem, width * sum(len(parts) for there, parts in ways(r, T, topo).values() if there == sem))

    def leave(deps, name):
        need("G", deps)
        there, parts = calls[name]
        moves = []
        for piece, hand, eng in parts:
            to = ids if hand is None else route(core, [hand], topo)[0]
            moves.append(RemoteDMATransfer(dst_ids=to, dma_engine_mask=eng, remote_sem=T.sem[there if hand is None else name],
                                           srcs=[piece], dsts=[piece for _ in to], alu_op=0))
            total["snt"] = total.get("snt", 0) + bin(eng).count("1")
        g.remote_dma_fused(moves, local_sem=T.sem.snt)

    ld = []
    for k in range(8):
        j, y = k // 2, k % 2
        ld.append(dma("Y" if k % 2 == 0 else "S", [], "ld%d" % k, T.raw[:, 8 * k:8 * k + 8, :],
                      T.bwt[y::2, 4096 * j:4096 * j + 4096]))
    lpat = dma("Y", [], "lpat", T.pat[:, :], T.pats[:, :])
    lst = dma("Y", [], "lst", T.sti[:, :], T.starts[:, :])

    fl = dict(allow_small_or_imprecise_dtypes=True)
    one = T.ones[:, 0:128]
    g_lp = run("G", [], g.iota, T.lp[:, :], [[0, 1]], 0, 1)
    g_m16 = run("G", [], g.iota, T.m16[:, :], [[0, 8], [1, 16]], 1, 0, **fl)
    t_one = run("V", [], v.memset, T.ones[:, :], 1.0)
    g_m8 = run("G", [], g.iota, T.m8[:, :], [[0, 16], [1, 8]], 0, 0, **fl)
    run("V", [], v.memset, T.onef[:, :], 1.0)
    t_c32 = run("V", [], v.memset, T.c32[:, :], 32.0)
    t = pick([t_one], T.t1[:, :], one, [[-16, 8], [0, 16]], Op.is_ge, 0.0, 0, 1)
    g_bm = pick([t], T.bm[:, :], T.t1[:, :], [[16, 8], [0, 16]], Op.is_ge, 0.0, 15, -1)
    t = pick([t_c32], T.t2[:, :], T.c32[:, :], [[-1, 128]], Op.is_ge, 0.0, 0, 1)
    s_wx = act([g_m16], T.wx[:, :], T.m16[:, :], Fn.Exp, scale=-math.log(32.0))

    lf = {n: T.lf[:, k:k + 1] for k, n in enumerate(
        ["lane", "y", "u", "odd", "x16", "sb", "sg", "u1", "bu", "bu1", "sl", "zs", "yy", "mb", "kc", "kn", "ky", "ko"])}
    g_gm = pick([t], T.gm[:, :], T.t2[:, :], [[4, 32], [0, 4]], Op.is_ge, 0.0, 3, -1)
    run("V", [g_lp], v.tensor_scalar, T.li[:, 0:1], T.lp[:, :], 15, None, Op.bitwise_and)
    ts([], T.li[:, 1:2], T.lp[:, :], 7, None, Op.bitwise_and)
    ts([], T.li[:, 2:3], T.lp[:, :], 3, 1, Op.arith_shift_right, Op.bitwise_and)
    t = ts([], T.li[:, 3:4], T.lp[:, :], 1, None, Op.bitwise_and)
    run("V", [], v.memset, T.vr[:, 0:1], 0.0)
    run("V", [], v.memset, T.vr[:, 129:132], 0.0)
    t_lf = run("V", [t], v.tensor_copy, T.lf[:, 0:4], T.li[:, 0:4])
    for name, src, a, b in [("x16", "lane", 0.0625, 0.0), ("sb", "u", -1.0, -3.0), ("sg", "u", -2.0, 1.0), ("u1", "u", -1.0, 1.0), ("bu", "u", -BIG, 0.0),
                            ("bu1", "u", BIG, -BIG), ("sl", "u", SEL, -SEL), ("zs", "u", -5 * SEL, SEL)]:
        ts([t_lf], lf[name], lf[src], a, b, Op.mult, Op.add)
    t_oh = ts([g_m16], T.oh[:, 0:8], T.m16[:, 0:8], -1.0, lf["lane"], Op.add, Op.is_equal)
    t_r = run("V", [], v.memset, T.zr[:, :], 1.0)
    t2 = ts([], lf["yy"], lf["y"], 1.0, lf["y"], Op.add, Op.mult)
    t = ts([g_m8, g_bm, t_oh], T.t1[:, :], T.m8[:, :], lf["sg"], lf["u"], Op.mult, Op.subtract)
    ts([], T.oh[:, 8:16], T.m8[:, 0:8], lf["y"], None, Op.is_equal)
    t_wb = tt([s_wx], T.wb[:, :], T.wx[:, :], T.bm[:, :], Op.mult)
    t_zr = run("V", [t_r], v.memset, T.zr[:, 0::8], 0.0)
    ts([t2], lf["mb"], lf["yy"], -2.0, 2.0, Op.mult, Op.add)
    t_yk = tt([t], T.yk[:, :], T.t1[:, :], T.bm[:, :], Op.mult)
    for j in range(4):
        g_wj = pick([t_wb], mat(T.wj, j), T.wb[:, :], [[0, 8], [1, 4], [0, 4]], Op.is_equal, 0.0, -j, 0)
    g_id = pick([], T.idm[:, :], one, [[-1, 128]], Op.is_equal, 0.0, 0, 1)
    g_swp = pick([], T.swp[:, :], one, [[-16, 8], [8, 2], [-1, 8]], Op.is_equal, 0.0, -8, 1)
    own = SW * rank
    for a, e in [(own + PARTS[1][3] - 8, own + PARTS[1][3]), (own + SW - 8, own + SW)]:
        t_pad = run("V", [], v.memset, T.ship[:, a:e], 0.0)
    fix = {n: T.fix[:, a:a + k] for n, a, k in [(-4.0, 0, 512), (4.0, 512, 64), (-16.0, 576, 64), (-32.0, 640, 64)]}
    for n in fix:
        s_fix = act([t_one], fix[n], T.ones[:, 0:fix[n].shape[1]], Fn.Copy, scale=n)
    t = act([g_gm], T.g1[:, 0:127], T.gm[:, 1:128], Fn.Copy, scale=-1.0)
    s_g1 = act([t], T.g1[:, 15::16], T.ones[:, 0:8], Fn.Copy, scale=0.0)

    def convert(k):
        h, at = k // 4, 16 * (k % 4)
        return run("V", [ld[k]], v.tensor_copy, T.half[:, 8 * h:8 * h + 8, at:at + 16], T.raw[:, 8 * k:8 * k + 8, :])

    def turn(h, deps):
        t_let.append(run("V", deps, v.transpose, T.let[:, 8 * h:8 * h + 8, :], T.half[:, 8 * h:8 * h + 8, :]))
        s_pw.append(act([t_let[h]], T.pw[:, 512 * h:512 * h + 512], T.let[:, 8 * h:8 * h + 8, :], Fn.Exp, scale=math.log(32.0)))

    def clamp(h, j):
        f = T.feat[:, B * j + 512 * h:B * j + 512 * h + 512]
        t = ts([s_pw[h]], f, T.pw[:, 512 * h:512 * h + 512], 32.0 ** (4 * j - 1), 32.0 ** (4 * j + 3), Op.max, Op.min)
        return mm([t, g_wj], bank(h), mat(T.wj, j), f, j == 0, j == 3)

    def whole(h, deps):
        return ts(deps, T.hq[:, 512 * h:512 * h + 512], bank(h), -4.0, None, Op.add)

    def digits(h, deps):
        cols = slice(512 * h, 512 * h + 512)
        t_nn.append(tt(deps, T.nn[:, cols], bank(h), T.hq[:, cols], Op.subtract))
        out = bank(2)[:, 64 * h:64 * h + 64]
        mm([s_nm, s_fix], out, T.nm[:, :], fix[-32.0], True, False)
        for i in range(8):
            t = mm([t_nn[h]], out, T.nm[:, :], nn(h, i), False, i == 7)
        return t

    def rises(h):
        e = bank(4 + h)
        for i in range(8):
            mm([], e[:, i::8], T.gm[:, :], nn(h, i), False, False)
            if i:
                mm([], e[:, i::8], T.g1[:, :], nn(h, i - 1), False, False)

    def offsets(h):
        e = bank(4 + h)
        mm([s_nm, s_fix], e, T.nm[:, :], fix[-4.0], True, False)
        mm([], e[:, 0::8], T.idm[:, :], fix[-16.0], False, False)
        mm([], e[:, 0::8], T.g1[:, :], fix[4.0], False, False)

    def nn(h, i):
        return T.nn[:, 512 * h + 64 * i:512 * h + 64 * i + 64]

    def keys_of(h):
        for i in range(8):
            t = act([t_oh], own_keys[:, 512 * h + i:512 * h + 512:8], T.let[:, 8 * h + i, :], Fn.Identity, bias=lf["x16"])
        leave([t], "k%d" % h)
        return t

    t_let, s_pw, t_nn = [], [], []
    own_keys = T.keyw[:, B * rank:B * rank + B]
    turn(0, [convert(k) for k in range(4)])
    keys_of(0)
    convert(4)
    convert(5)
    mm([s_g1, g_id], bank(3)[:, 0:128], T.idm[:, :], T.gm[:, :], True, False)
    t = mm([], bank(3)[:, 0:128], T.idm[:, :], T.g1[:, :], False, True)
    s_nm = act([t], T.nm[:, :], bank(3)[:, 0:128], Fn.Copy)
    clamp(0, 0)
    offsets(0)
    turn(1, [convert(k) for k in range(6, 8)])
    t_key = keys_of(1)
    for u in range(2):
        g_wu = pick([], mat(T.wu, u), one, [[-16, 8], [0, 2], [-1, 8]], Op.is_equal, 0.0, -8 * u, 1)
    t = pick([], T.t3[:, :], T.onef[:, :], [[-16, 8], [0, 16]], Op.is_ge, 0.0, 0, 1)
    g_lt = pick([t], T.lt[:, :], T.t3[:, :], [[1, 128]], Op.is_gt, 0.0, 0, -1)
    t_d0 = [clamp(0, j) for j in range(1, 4)]
    for q in range(8):
        s_xq = act([g_bm], mat(T.xq, q), T.bm[:, :], Fn.Copy, scale=T.oh[:, q:q + 1])
    for q in range(8):
        act([t_yk], mat(T.mq, q), T.yk[:, :], Fn.Copy, scale=T.oh[:, 8 + q:9 + q])
    act([], T.n4[:, :], T.idm[:, :], Fn.Copy, scale=-4.0)
    t_zt = [act([], T.zt[:, ZW * k:ZW * k + ZW], T.ones[:, :], Fn.Copy, scale=lf["bu" if k % 2 else "bu1"]) for k in range(2)]
    s_nsw = act([g_swp], T.nsw[:, :], T.swp[:, :], Fn.Copy, scale=-1.0)
    act([], T.b16[:, :], T.bm[:, :], Fn.Copy, scale=0.0625)
    s_b32 = act([], T.b32[:, :], T.bm[:, :], Fn.Copy, scale=0.03125)
    clamp(1, 0)
    clamp(1, 1)
    offsets(1)
    run("V", [lpat], v.tensor_copy, T.cl[:, 0:128], T.pat[:, 0:128])
    t_h0 = whole(0, t_d0)
    clamp(1, 2)
    t_d1 = clamp(1, 3)
    digits(0, [t_h0])
    t_cl = run("V", [], v.tensor_copy, T.cl[:, 128:256], T.pat[:, 128:256])
    rises(0)
    t_h1 = whole(1, [t_d1])
    t = ts([lst], T.s1[:, :], T.sti[:, :], 15, None, Op.bitwise_and)
    t_sb = digits(1, [t_h1])
    ts([], T.s2[:, :], T.sti[:, :], 4, None, Op.arith_shift_right)
    t_s3 = ts([], T.s3[:, :], T.pat[:, 0:32], 8.0, float(STR), Op.is_ge, Op.mult)
    t_kc = ts([t], T.kc[:, :], T.s1[:, :], 0.0625, None, Op.mult)
    t_vr = run("V", [t_sb], v.tensor_tensor_scan, T.vr[:, 1:129], one, bank(2)[:, 0:128], 0.0, Op.mult, Op.add)
    t_tot = run("V", [t_vr], v.tensor_copy, T.tot[:, 4 * rank:4 * rank + 4], T.vr[:, 128:132])
    leave([t_tot], "tv")
    g_le = pick([], T.le[:, :], T.t3[:, :], [[1, 128]], Op.is_ge, 0.0, 0, -1)
    for buf, a, e, n in [(T.keyw, NB, STR, 1024), (T.keyw, STR + NB, W, 1024), (T.base, NB + 1, STR, 0), (T.base, STR + NB + 1, W, 0)]:
        t_fill = run("G", [], g.iota, buf[:, a:e], [[0, e - a]], n, 0, **fl)

    for u in range(2):
        t = mm([t_cl, g_wu], bank(7)[:, u::2], mat(T.wu, u), T.cl[:, :], True, True)
    s_cd = act([t], T.cd[:, :], bank(7), Fn.Copy)
    t_ch = act([], T.ch[:, :], bank(7), Fn.Sign, bias=-7.5)
    rises(1)
    mm([s_cd], bank(6), T.idm[:, :], T.cd[:, :], True, False)
    t = mm([t_ch], bank(6), T.n4[:, :], T.ch[:, :], False, True)
    act([], T.ih[:, :], T.idm[:, :], Fn.Copy, scale=STR / 2)
    s_neg = act([], T.neg[:, :], T.idm[:, :], Fn.Copy, scale=-1.0)
    t_zt += [ts([], T.zt[:, ZW * k:ZW * k + ZW], T.ones[:, :], lf["bu" if k % 2 else "bu1"], None, Op.mult) for k in range(2, 4)]
    s_sq = act([t], T.sq[:, :], bank(6), Fn.Square, bias=lf["sb"])
    t_m = []

    def masks(st):
        for q in range(8):
            t = mm([s_sq, t_nn[1]] + t_m[st - 2:st - 1], bank(st % 2)[:, q::8], mat(T.mq, q), T.sq[:, 64 * st:64 * st + 64], True, True)
        t_m.append(act([t], T.msk[:, 512 * st:512 * st + 512], bank(st % 2), Fn.Relu, scale=2.0, bias=lf["mb"]))

    t_z = run("V", [], v.memset, T.zs[:, :], -4 * SEL)
    ts([], lf["kc"], lf["odd"], -0.5, 0.46875, Op.mult, Op.add)
    ts([], lf["kn"], lf["odd"], -0.5, None, Op.mult)
    t = ts([], lf["ky"], lf["odd"], 0.5, lf["sl"], Op.mult, Op.add)
    t_zs = ts([t_z], T.zs[:, 1::2], T.onef[:, 0:32], lf["zs"], None, Op.mult)
    t_kap = ts([t], lf["ko"], lf["ky"], STR / 2 - 0.46875, None, Op.add)
    kap = {n: [lf["k" + n]] * 2 for n in "cnyo"}
    for x in range(2):
        t2 = tt([t_s3], T.s4[:, 32 * x:32 * x + 32], T.s2[:, 32 * x:32 * x + 32], T.s3[:, :], Op.add)
    t = run("V", [t2], v.tensor_copy, T.off[:, 0:64], T.s4[:, :])
    t_of, t_kl = [t, t], []
    t_dup = [run("V", [t_key], v.tensor_copy, T.keyw[:, STR + B * rank:STR + B * rank + B], own_keys)]
    for st in range(EARLY):
        masks(st)

    cols = T.tot[:, 0:4 * R:4]
    if rank:
        mm([("tin", width * (R - 1)), t_tot, g_le], bank(3)[:, 0:rank], T.le[:, :], cols[:, 0:rank], True, True)
    t = mm([("tin", width * (R - 1)), t_tot, g_le], bank(3)[:, rank:R], T.lt[:, :], cols[:, rank:R], True, True)
    t = run("V", [t], v.tensor_reduce, T.init[:, :], bank(3)[:, 0:R], AxisListType.X, Op.add)
    masks(EARLY)
    val = bank(2)[:, 256:385]
    t_hb = ts([t], T.hb[:, 0:129], T.vr[:, 0:129], T.init[:, :], 256.0, Op.add, Op.max)
    t = ts([], val, T.vr[:, 0:129], T.init[:, :], None, Op.add)
    t_rb = tt([t], T.rb[:, 0:129], val, T.hb[:, 0:129], Op.subtract)
    s_dh = []
    for b0, n, at, low, end in PARTS:
        a, k = b0 // 8, (n + 7) // 8
        out = bank(6)[:, a:a + k]
        mm([t_hb, s_nsw, s_sq], out, T.swp[:, :], T.hb[:, a:a + k], True, False)
        t = mm([], out[:, 1:], T.nsw[:, :], T.hb[:, a:a + k - 1], False, True)
    t_e2 = [mm([t_rb], bank(4 + h)[:, 0::8], T.idm[:, :], T.rb[:, 64 * h:64 * h + 64], False, True) for h in range(2)]
    for b0, n, at, low, end in PARTS:
        a, k = b0 // 8, (n + 7) // 8
        s_dh.append(act([t, t_pad], T.ship[:, own + at:own + at + k], bank(6)[:, a:a + k], Fn.Copy))
    lo_a, lo_b = own + PARTS[0][3], own + PARTS[1][3]
    scan = v.tensor_tensor_scan
    run("V", [t_pad, t_rb], v.tensor_copy, T.ship[:, lo_b + B - HC:lo_b + B - HC + 1], T.rb[:, 128:129])
    cuts = sorted({0, 512, HC, B})
    for a, e in zip(cuts, cuts[1:]):
        to = lo_a + a if a < HC else lo_b + a - HC
        t_lb = run("V", [t_e2[a // 512], t_zr], scan, T.ship[:, to:to + e - a], T.zr[:, 0:e - a], T.pb[:, a:e], 0.0, Op.mult, Op.add)
        if e == HC:
            t_la = t_lb
            leave([t_la, s_dh[0]], "la")
    leave([t_lb, s_dh[1]], "lb")

    used = {}

    def unfold(r, part, slot, deps):
        b0, n, at, low, end = PARTS[part]
        n -= part == 1 and r < R - 1
        k = (n + 7) // 8
        for chi in range(2):
            z = T.zt[:, ZW * (2 * slot + chi):ZW * (2 * slot + chi) + n]
            t = act(deps + [t_zt[2 * slot + chi]] + used.get((slot, chi), []), z[:, 0::8], T.ship[:, SW * r + at:SW * r + at + k], Fn.Identity,
                    scale=lf["u1" if chi else "u"], bias=lf["bu" if chi else "bu1"])
            to = T.base[:, STR * chi + B * r + b0:STR * chi + B * r + b0 + n]
            t = run("V", deps + [t], scan, to, z, T.ship[:, SW * r + low:SW * r + low + n], 0.0, Op.add, Op.max)
            used[slot, chi] = [t]
        return t

    unfold(rank, 0, 0, [t_la, s_dh[0]])
    unfold(rank, 1, 1, [t_lb, s_dh[1]])
    for q in range(8):
        t_e = pick([s_b32], mat(T.e32, q), T.b32[:, :], [[0, 16], [1, 8]], Op.is_equal, 0.0, -q, 0)
    for q in range(8):
        if any(e == "V" and q % k == a for x in range(2) for e, a, k in SHARE[x]):
            t_e = pick([], mat(T.e16, q), T.b16[:, :], [[0, 16], [1, 8]], Op.is_equal, 0.0, -q, 0)
    for st in range(EARLY + 1, 8):
        masks(st)
    for x in range(2):
        for u in range(2):
            out = bank(7)[:, 64 * x + u:64 * x + 64:2]
            mm([t_kc, s_cd], out, mat(T.wu, u), T.kc[:, 32 * x:32 * x + 32], True, False)
            t = mm([], out, mat(T.wu, u), T.cl[:, 0:32], False, True)
    for x in range(2):
        t_kl.append(act([t, t_kap], T.kl[:, 64 * x:64 * x + 64], bank(7)[:, 64 * x:64 * x + 64], Fn.Identity, bias=kap["n"][x]))
    s_clb = run("V", [t_kap, s_cd], v.tensor_scalar, T.clb[:, 64:512], T.cd[:, 64:512], kap["c"][0], None, Op.add)
    for k in range(1, R):
        r = (rank - k) % R
        t_dup = [run("V", [landed("kin%d" % r)], v.tensor_copy, T.keyw[:, STR + B * r:STR + B * r + B], T.keyw[:, B * r:B * r + B])]
    for n, (part, k) in enumerate([(1, 1), (1, 2), (0, 1), (0, 2), (1, 3), (0, 3)]):
        r = (rank - k) % R
        t_base = [unfold(r, part, n % 2, [landed("%s%d" % ("lb" if part else "la", r))])]

    P = [bank(6)[:, 0:64], bank(7)[:, 0:64]]
    banks = [{"V": bank(0), "S": bank(1)}, {"V": bank(2), "S": bank(3)}]
    lay = []
    for x in range(2):
        at, d, parts = {"V": 0, "S": 0}, {}, []
        for e, a, k in SHARE[x]:
            n = 512 // k
            parts.append((e, a, k, at[e], n))
            for q in range(a, 8, k):
                d[q] = (e, slice(at[e] + q // k, at[e] + n, 8 // k))
            at[e] += n
        lay.append((d, parts, at))
    xs = [{"V": T.xs[:, 512 * x:512 * x + 512], "S": T.xs[:, 512 * x + lay[x][2]["V"]:512 * x + 512]} for x in range(2)]
    kg = [T.kg[:, 512 * x:512 * x + 512] for x in range(2)]
    ym = [T.ym[:, 512 * x:512 * x + 512] for x in range(2)]
    tk = [{}, {}]

    def offs(x, st):
        at = 64 * (st % 2) + 32 * x
        return T.off[:, at:at + 32]

    def keys(x, st):
        tk[x]["kg"] = act([t_of[x], t_fill] + t_dup, kg[x], T.keyw[:, 0:W].indirect(offs(x, st)), Fn.Copy)

    def bases(x, st, a, e):
        tk[x]["ym"] = tt([t_of[x], t_m[st], t_fill] + t_base, ym[x][:, 16 * a:16 * e], T.base[:, 0:W].indirect(offs(x, st)[:, a:e]),
                         T.msk[:, 512 * st + 16 * a:512 * st + 16 * e], Op.mult)

    def spread(x, st, deps=()):
        begun = set()
        for q in range(8):
            e, c = lay[x][0][q]
            alone = e == "V"
            tk[x]["sp"] = mm([t_kl[x]] + list(deps), banks[x][e][:, c], mat(T.xq, q), T.kl[:, 64 * x:64 * x + 64], alone or e not in begun, alone)
            begun.add(e)
        if st < 7:
            mm([t_ch], P[x], T.ih[:, :], T.ch[:, 64 * st + 64:64 * st + 128], True, False)

    def minus(x):
        mine = [p for p in lay[x][1] if p[0] == "S"]
        for e, a, k, at, n in mine:
            tk[x]["ng"] = mm([tk[x]["kg"], s_neg], banks[x]["S"][:, at:at + n], T.neg[:, :], kg[x][:, a::k], False, at == mine[-1][3])

    def compare(x, e):
        n = lay[x][2]["S"]
        if e == "S" and n:
            tk[x]["S"] = act([tk[x]["ng"]], xs[x]["S"][:, 0:n], banks[x]["S"][:, 0:n], Fn.Sign, bias=0.46875)
        for e2, a, k, at, n in lay[x][1]:
            if e == e2 == "V":
                tk[x]["V"] = tt([tk[x]["kg"], tk[x]["sp"]], xs[x]["V"][:, at:at + n], kg[x][:, a::k], banks[x]["V"][:, at:at + n], Op.is_lt)

    def sum_bases(x, st):
        for q in range(8):
            mm([tk[x]["ym"], t_e], P[x], mat(T.e32, q), ym[x][:, q::8], st == 7 and q == 0, False)

    def sum_signs(x, e):
        qs = [q for q in range(8) if lay[x][0][q][0] == e]
        for q in qs:
            tk[x]["P"] = mm([tk[x][e]], P[x], mat(T.e32 if e == "S" else T.e16, q), xs[x][e][:, lay[x][0][q][1]], False,
                            q == qs[-1] and (e == "S" or len(qs) == 8))

    def choose(x, st):
        sel, oi = T.sel[:, 64 * x:64 * x + 64], T.oi[:, 64 * x:64 * x + 64]
        t = run("V", [tk[x]["P"], t_zs], scan, sel, T.zs[:, :], P[x], 0.0, Op.add, Op.max)
        if st < 7:
            t2 = tt([s_clb], oi, P[x], T.clb[:, 64 * st + 64:64 * st + 128], Op.subtract)
            t_of[x] = ts([t], offs(x, st + 1), sel[:, 1::2], kap["o"][x], None, Op.add)
            t_kl[x] = tt([t2], T.kl[:, 64 * x:64 * x + 64], P[x], oi, Op.subtract)
        else:
            t_of[x] = ts([t], T.yo[:, 32 * x:32 * x + 32], sel[:, 1::2], kap["y"][x], 16.0, Op.add, Op.mult)

    A, Z = 0, 1
    for st in range(8):
        keys(A, st)
        bases(A, st, 0, 16)
        if st:
            sum_signs(Z, "S")
            choose(Z, st - 1)
        spread(A, st, [] if st else [t_m[7], t_kl[1], t_lb, s_neg])
        keys(Z, st)
        bases(A, st, 16, 32)
        spread(Z, st)
        minus(A)
        compare(A, "V")
        sum_bases(A, st)
        sum_signs(A, "V")
        minus(Z)
        compare(A, "S")
        bases(Z, st, 0, 32)
        compare(Z, "V")
        sum_signs(A, "S")
        compare(Z, "S")
        sum_bases(Z, st)
        sum_signs(Z, "V")
        choose(A, st)
    sum_signs(Z, "S")
    choose(Z, 7)
    dma("Y", t_of, "out", T.y[:, :], T.yo[:, :])

    for sem in ["cV", "cS", "cP", "cG", "out", "snt"]:
        need("G", [(sem, total[sem])])
